import numpy as np
import ml_dtypes


def mxq(x, axis, fmt="e4m3"):
    dtype, down = {"e4m3": (ml_dtypes.float8_e4m3fn, 7), "e5m2": (ml_dtypes.float8_e5m2, 14)}[fmt]
    v = np.moveaxis(np.asarray(x, np.float32).astype(ml_dtypes.bfloat16).astype(np.float64), axis, -1)
    blocks = v.reshape(v.shape[:-1] + (-1, 32))
    amax = np.abs(blocks).max(-1, keepdims=True)
    byte = np.maximum(np.where(amax > 0, np.frexp(amax)[1] - 1 + 127, 0) - down, 1)
    scale = np.exp2(byte - 127.0)
    codes = (blocks / scale).astype(np.float32).astype(dtype).astype(np.float64)
    return np.moveaxis((codes * scale).reshape(v.shape), -1, axis)


WIDE = False


def mx_kscale(k):
    if not WIDE:
        return np.ones(k)
    levels = np.array([24, -24, 12, -12, 0])
    if k % 512:
        return np.exp2(np.random.permutation(np.resize(levels, k // 32))).repeat(32)
    a = np.empty((k // 512, 16))
    for p in range(k // 512):
        a[p, :8] = np.random.permutation(np.resize(levels, 8))
        for g in range(8):
            far = levels[np.abs(levels - a[p, g]) >= 10]
            a[p, g + 8] = far[np.random.randint(len(far))]
    return np.exp2(a.ravel()).repeat(32)


def f64(x):
    return np.asarray(x).astype(np.float64)


def striped(idx):
    return np.tile(idx.reshape(-1, 16).T, (8, 1)).astype(np.uint16)


def unstriped(offs):
    return offs[:16].T.reshape(-1).astype(np.int64)


E2M1 = np.array([0.0, 0.5, 1.0, 1.5, 2.0, 3.0, 4.0, 6.0, -0.0, -0.5, -1.0, -1.5, -2.0, -3.0, -4.0, -6.0])


def pack_weight(w, fmt):
    k, n = w.shape
    w = f64(np.asarray(w, np.float32).astype(ml_dtypes.bfloat16)).reshape(k // 32, 32, n)
    amax = np.abs(w).max(1)
    if fmt == "e4m3":
        byte = np.frexp(amax)[1] - 1 + 127 - 7
    else:
        mant, ex = np.frexp(amax / 6.0)
        byte = np.where(mant > 0.5, ex, ex - 1) + 127
    byte = np.clip(np.where(amax > 0, byte, 1), 1, 254)
    scaled = (w * np.exp2(127.0 - byte)[:, None, :]).reshape(k, n).astype(np.float32)
    by_word = np.ascontiguousarray(scaled.reshape(k // 512, 128, 4, n).transpose(0, 1, 3, 2))
    if fmt == "e4m3":
        words = by_word.astype(ml_dtypes.float8_e4m3fn).view(np.uint8)
    else:
        c = by_word.astype(ml_dtypes.float4_e2m1fn).view(np.uint8) & 0xF
        words = (c[..., 0::2] | (c[..., 1::2] << 4)).reshape(k // 512, 128, 2 * n)
    return np.ascontiguousarray(words), np.ascontiguousarray(byte.astype(np.uint8).reshape(k // 512, 16, n))


def unpack_weight(words, scales, fmt):
    g, _, n = scales.shape
    words = np.ascontiguousarray(words).reshape(g, 128, n, -1)
    if fmt == "e4m3":
        vals = words.view(ml_dtypes.float8_e4m3fn).astype(np.float64)
    else:
        nib = np.empty((g, 128, n, 4), np.uint8)
        nib[..., 0::2] = words & 0xF
        nib[..., 1::2] = words >> 4
        vals = E2M1[nib]
    vals = vals * np.repeat(np.exp2(scales.astype(np.float64) - 127.0), 8, axis=1)[..., None]
    return vals.transpose(0, 1, 3, 2).reshape(g * 512, n)


def pack_table4(v):
    words, scales = pack_weight(v, "e2m1")
    g, t = words.shape[0] // 2, v.shape[1]
    return np.ascontiguousarray(words.reshape(g, 2, 128, t, 2).transpose(0, 2, 3, 1, 4).reshape(g, 128, t, 4)), scales


def unpack_table4(words, scales):
    g, _, t, _ = words.shape
    return unpack_weight(words.reshape(g, 128, t, 2, 2).transpose(0, 3, 1, 2, 4).reshape(2 * g, 128, 2 * t), scales, "e2m1")


def sigm(f):
    return 1.0 / (1.0 + np.exp(-np.maximum(f, -700.0)))


K, N, T, J = 1024, 512, 2048, 1024


def setup_inputs():
    n = np.random.standard_normal
    s = mx_kscale(K)[:, None]
    p_tab = pack_table4(n((K, T)) * s)
    p_wa = pack_weight(n((K, N)) / np.sqrt(2 * K) / s, "e4m3")
    p_wc = pack_weight(n((K, N)) / np.sqrt(K) / s, "e2m1")
    return {
        "tab_words": p_tab[0],
        "tab_scales": p_tab[1],
        "wa_words": p_wa[0],
        "wa_scales": p_wa[1],
        "wb": (n((K, N)) / np.sqrt(2 * K) / s).astype(np.float32),
        "wc_words": p_wc[0],
        "wc_scales": p_wc[1],
        "wo": (n((K, N)) / np.sqrt(K) / s).astype(np.float32),
        "rT": (n((N, T))).astype(np.float32),
        "wgo": np.tile(np.random.uniform(0.5, 2.0, J), (128, 1)).astype(np.float32),
        "offs": striped(np.random.permutation(T)[:J]),
        "offs2": striped(np.random.permutation(T)[:J]),
    }


def reference(tab_words, tab_scales, wa_words, wa_scales, wb, wc_words, wc_scales, wo, rT, wgo, offs, offs2):
    idx = unstriped(offs)
    idx2 = unstriped(offs2)
    tab_ = unpack_table4(tab_words, tab_scales)[:, idx]
    tabb_ = unpack_table4(tab_words, tab_scales)[:, idx2]
    wa_ = unpack_weight(wa_words, wa_scales, "e4m3")
    wb_ = mxq(f64(wb), 0, "e4m3")
    za = wa_.T @ tabb_ + wb_.T @ tab_
    eta = sigm(za)
    wc_ = unpack_weight(wc_words, wc_scales, "e2m1")
    ms = wc_.T @ tab_
    wo_ = mxq(f64(wo), 0, "e4m3")
    ow = wo_.T @ tabb_
    out = np.zeros((N, T))
    out[:, idx2] = f64(wgo)[0] * (ow + eta * ms + f64(rT)[:, idx2])
    return out

@@ -1,0 +1,213 @@
+from contextlib import ExitStack
+
+import concourse.mybir as mybir
+from concourse.masks import make_identity
+
+K, N, T, J = 1024, 512, 2048, 1024
+FLOPS = 4 * 2 * K * N * J
+
+F32 = mybir.dt.float32
+BF16 = mybir.dt.bfloat16
+I32 = mybir.dt.int32
+U32 = mybir.dt.uint32
+U16 = mybir.dt.uint16
+U8 = mybir.dt.uint8
+FP8X4 = mybir.dt.float8_e4m3fn_x4
+FP4X4 = mybir.dt.float4_e2m1fn_x4
+MULT = mybir.AluOpType.mult
+ADD = mybir.AluOpType.add
+COPY = mybir.ActivationFunctionType.Copy
+SIGMOID = mybir.ActivationFunctionType.Sigmoid
+
+P = 128
+PACK = 4
+PASSES = K // (P * PACK)
+QUADS = 4
+EDGE_TILES = J // P
+ROW_TILES = N // P
+HALF = 512
+PAGES = 3
+TGT, SRC = 0, 1
+
+
+def tile_list_rgg_ownL_kernel(
+    tc, tab_words, tab_scales, wa_words, wa_scales, wb, wc_words, wc_scales, wo, rT, wgo, offs, offs2, out
+):
+    nc = tc.nc
+    with ExitStack() as ctx:
+        keep = ctx.enter_context(tc.tile_pool(name="keep", bufs=1))
+        ring = ctx.enter_context(tc.tile_pool(name="ring", bufs=2))
+        psum = ctx.enter_context(tc.psum_pool(name="psum", bufs=2))
+
+        tgt_list = keep.tile([P, J // 16], U16, name="tgt_list")
+        src_list = keep.tile([P, J // 16], U16, name="src_list")
+        lists = (tgt_list, src_list)
+        tab_s = keep.tile([P, T], U8, name="tab_s", align_bytes=64)
+        tab_w = keep.tile([P, T], U32, name="tab_w", align_bytes=64)
+        got_s = keep.tile([P, 2 * J], U8, name="got_s", align_bytes=64)
+        moved_s = keep.tile([P, 2 * J], U8, name="moved_s", align_bytes=64)
+        wa_w = keep.tile([P, PASSES, N], U32, name="wa_w", align_bytes=64)
+        wc_w = keep.tile([P, PASSES, 2 * N], U8, name="wc_w", align_bytes=64)
+        wa_s = keep.tile([P, PASSES, N], U8, name="wa_s", align_bytes=64)
+        wc_s = keep.tile([P, PASSES, N], U8, name="wc_s", align_bytes=64)
+        wgo_rows = keep.tile([P, J], F32, name="wgo_rows")
+        wgo_cols = keep.tile([P, EDGE_TILES], F32, name="wgo_cols")
+        ident = keep.tile([P, P], F32, name="ident")
+        pages = [keep.tile([P, T], F32, name="page%d" % r) for r in range(PAGES)]
+
+        make_identity(nc, ident[:])
+        warm = keep.tile([P, 1], F32, name="warm")
+        nc.scalar.activation(warm[:], ident[:, 0:1], SIGMOID)
+        nc.vector.memset(tab_s[:].bitcast(I32), 0)
+        nc.vector.memset(moved_s[:].bitcast(I32), 0)
+        nc.vector.memset(wa_s[:].bitcast(I32), 0)
+        nc.vector.memset(wc_s[:].bitcast(I32), 0)
+
+        nc.sync.dma_start(tgt_list[:], offs2)
+        nc.sync.dma_start(src_list[:], offs)
+        for q in range(QUADS):
+            nc.sync.dma_start(
+                tab_s[:].bitcast(I32)[32 * q : 32 * q + 4 * PASSES, :],
+                tab_scales.bitcast(I32)[:, 4 * q : 4 * q + 4, :],
+            )
+        nc.sync.dma_start(tab_w[:].bitcast(I32), tab_words[0].rearrange("p t b -> p (t b)").bitcast(I32))
+
+        def load_scales(plane, rows):
+            for q in range(QUADS):
+                nc.sync.dma_start(
+                    plane[:].bitcast(I32)[32 * q : 32 * q + 4, :, :],
+                    rows.bitcast(I32)[:, 4 * q : 4 * q + 4, :].rearrange("a r w -> r a w"),
+                )
+
+        def load_raw(w, a):
+            raw = ring.tile([P, PACK, N], F32, name="raw", bufs=4)
+            nc.sync.dma_start(raw[:], w[512 * a : 512 * (a + 1), :].rearrange("(p i) n -> p i n", i=PACK))
+            return raw
+
+        def weave(raw):
+            woven = ring.tile([P, N, PACK], BF16, name="woven", align_bytes=64, bufs=4)
+            nc.scalar.copy(
+                woven[:].rearrange("p (c u) i -> p c i u", u=4),
+                raw[:].rearrange("p i (c u) -> p c i u", u=4),
+            )
+            return woven
+
+        def quantise(woven, name):
+            codes = keep.tile([P, N], U32, name=name + "_w", align_bytes=64)
+            plane = keep.tile([P, N], U8, name=name + "_s", align_bytes=64)
+            nc.vector.quantize_mx(
+                out=codes[:].bitcast(FP8X4), scales=plane[:], in_=woven[:].rearrange("p n i -> p (n i)")
+            )
+            return codes[:].bitcast(FP8X4), plane[:]
+
+        def load_state(r):
+            state = ring.tile([P, T], F32, name="state", bufs=3)
+            nc.sync.dma_start(state[:], rT[P * r : P * (r + 1), :])
+            return state
+
+        def gather_state(state, r):
+            own = keep.tile([P, J], F32, name="own%d" % r)
+            nc.vector.tensor_tensor(own[:], state[:].indirect(tgt_list[:]), wgo_rows[:], MULT)
+            return own
+
+        raw_o = [load_raw(wo, a) for a in range(PASSES)]
+        raw_b = [load_raw(wb, 0)]
+        load_scales(wa_s, wa_scales)
+        nc.sync.dma_start(wa_w[:].bitcast(I32), wa_words.rearrange("a p n b -> p a (n b)").bitcast(I32))
+        load_scales(wc_s, wc_scales)
+        nc.sync.dma_start(wc_w[:].bitcast(I32), wc_words.rearrange("a p m -> p a m").bitcast(I32))
+        raw_b.append(load_raw(wb, 1))
+        nc.sync.dma_start(wgo_rows[:], wgo)
+        states = [load_state(r) for r in range(3)]
+
+        for side in (TGT, SRC):
+            nc.vector.tensor_copy(got_s[:, side * J : (side + 1) * J], tab_s[:].indirect(lists[side][:]))
+        nc.scalar.dma_start(moved_s[:].bitcast(I32)[0 : P - 4, :], got_s[:].bitcast(I32)[4:P, :])
+        parted = []
+        for side in (TGT, SRC):
+            got_w = ring.tile([P, J], U32, name="got_w", align_bytes=64)
+            nc.vector.tensor_copy(got_w[:], tab_w[:].indirect(lists[side][:]))
+            halves = keep.tile([P, PASSES, 2 * J], U8, name="parted%d" % side, align_bytes=64)
+            nc.vector.tensor_copy(
+                halves[:].bitcast(U16), got_w[:].bitcast(U16).rearrange("p (j a) -> p a j", a=PASSES)
+            )
+            parted.append(halves)
+
+        for page in pages:
+            nc.vector.memset(page[:].bitcast(I32), 0)
+
+        def nodes(side, a, e):
+            codes = parted[side][:, a, 2 * P * e : 2 * P * (e + 1)].bitcast(FP4X4)
+            plane = (got_s, moved_s)[a][:, side * J + P * e : side * J + P * (e + 1)]
+            return codes, plane
+
+        wo_q = [quantise(weave(raw_o[a]), "wo%d" % a) for a in range(PASSES)]
+        wb_q = [quantise(weave(raw_b[a]), "wb%d" % a) for a in range(PASSES)]
+        wa_q = [(wa_w[:, a, :].bitcast(FP8X4), wa_s[:, a, :]) for a in range(PASSES)]
+        wc_q = [(wc_w[:, a, :].bitcast(FP4X4), wc_s[:, a, :]) for a in range(PASSES)]
+
+        for h in range(J // HALF):
+            turned = psum.tile([P, HALF], F32, name="sums")
+            for c in range(HALF // P):
+                e = h * (HALF // P) + c
+                nc.tensor.transpose(turned[:, P * c : P * (c + 1)], wgo_rows[:, P * e : P * (e + 1)], ident[:])
+            nc.scalar.copy(wgo_cols[:, 4 * h : 4 * h + 4], turned[:, 0:HALF:P])
+
+        owns = [gather_state(states[0], 0)]
+        states.append(load_state(3))
+
+        def product(bank, terms, e):
+            steps = [(side, w, a) for side, w in terms for a in range(PASSES)]
+            for s, (side, w, a) in enumerate(steps):
+                codes, plane = nodes(side, a, e)
+                nc.tensor.matmul_mx(
+                    out=bank[:], lhsT=codes, lhsT_scale=plane, rhs=w[a][0], rhs_scale=w[a][1],
+                    start=(s == 0), stop=(s == len(steps) - 1),
+                )
+
+        def edge_tile(e):
+            za = psum.tile([P, N], F32, name="za")
+            product(za, ((TGT, wa_q), (SRC, wb_q)), e)
+            ms = psum.tile([P, N], F32, name="ms")
+            product(ms, ((SRC, wc_q),), e)
+            ow = psum.tile([P, N], F32, name="ow")
+            product(ow, ((TGT, wo_q),), e)
+            eta = ring.tile([P, N], F32, name="eta")
+            nc.scalar.activation(eta[:], za[:], SIGMOID)
+            kept = keep.tile([P, N], F32, name="kept%d" % e)
+            nc.scalar.activation(kept[:], ow[:], COPY, scale=wgo_cols[:, e : e + 1])
+            gated = keep.tile([P, N], F32, name="gated%d" % e)
+            nc.vector.scalar_tensor_tensor(gated[:], ms[:], wgo_cols[:, e : e + 1], eta[:], MULT, MULT)
+            return kept, gated
+
+        def place(h, r, terms):
+            sums = psum.tile([P, HALF], F32, name="sums")
+            for c in range(HALF // P):
+                for s, term in enumerate(terms[c]):
+                    nc.tensor.matmul(
+                        sums[:, P * c : P * (c + 1)], term[:, P * r : P * (r + 1)], ident[:],
+                        start=(s == 0), stop=(s == 1), is_transpose=True,
+                    )
+            update = ring.tile([P, HALF], F32, name="update", bufs=4)
+            nc.scalar.copy(update[:], sums[:])
+            cols = HALF // 16
+            nc.vector.tensor_tensor(
+                pages[r % PAGES][:].indirect(tgt_list[:, cols * h : cols * (h + 1)]),
+                update[:], owns[r][:, HALF * h : HALF * (h + 1)], ADD,
+            )
+
+        terms = []
+        for h in range(J // HALF):
+            terms.append([])
+            for c in range(HALF // P):
+                terms[h].append(edge_tile(h * (HALF // P) + c))
+                if h == 0 and c > 0:
+                    owns.append(gather_state(states[c], c))
+            for r in range(PAGES):
+                place(h, r, terms[h])
+                if h == J // HALF - 1:
+                    nc.sync.dma_start(out[P * r : P * (r + 1), :], pages[r][:])
+        for r in range(PAGES, ROW_TILES):
+            for h in range(J // HALF):
+                place(h, r, terms[h])
+            nc.sync.dma_start(out[P * r : P * (r + 1), :], pages[r % PAGES][:])

@@ -26,7 +26,7 @@ QUADS = 4
 EDGE_TILES = J // P
 ROW_TILES = N // P
 HALF = 512
-PAGES = 3
+PAGES = 4
 TGT, SRC = 0, 1
 
 
@@ -55,13 +55,15 @@ def tile_list_rgg_ownL_kernel(
         ident = keep.tile([P, P], F32, name="ident")
         pages = [keep.tile([P, T], F32, name="page%d" % r) for r in range(PAGES)]
 
+        for plane in (tab_s, wa_s, wc_s, moved_s):
+            nc.gpsimd.memset(plane[:].bitcast(I32), 0)
         make_identity(nc, ident[:])
-        warm = keep.tile([P, 1], F32, name="warm")
-        nc.scalar.activation(warm[:], ident[:, 0:1], SIGMOID)
-        nc.vector.memset(tab_s[:].bitcast(I32), 0)
-        nc.vector.memset(moved_s[:].bitcast(I32), 0)
-        nc.vector.memset(wa_s[:].bitcast(I32), 0)
-        nc.vector.memset(wc_s[:].bitcast(I32), 0)
+        warm = keep.tile([P, 16], F32, name="warm")
+        nc.vector.memset(warm[:, 0:1], 0.0)
+        nc.scalar.activation(warm[:, 8:9], warm[:, 0:1], SIGMOID)
+        nc.vector.memset(pages[0][:].bitcast(I32), 0)
+        for page in pages[1:]:
+            nc.gpsimd.memset(page[:].bitcast(I32), 0)
 
         nc.sync.dma_start(tgt_list[:], offs2)
         nc.sync.dma_start(src_list[:], offs)
@@ -133,9 +135,6 @@ def tile_list_rgg_ownL_kernel(
             )
             parted.append(halves)
 
-        for page in pages:
-            nc.vector.memset(page[:].bitcast(I32), 0)
-
         def nodes(side, a, e):
             codes = parted[side][:, a, 2 * P * e : 2 * P * (e + 1)].bitcast(FP4X4)
             plane = (got_s, moved_s)[a][:, side * J + P * e : side * J + P * (e + 1)]
@@ -196,18 +195,17 @@ def tile_list_rgg_ownL_kernel(
                 update[:], owns[r][:, HALF * h : HALF * (h + 1)], ADD,
             )
 
-        terms = []
-        for h in range(J // HALF):
-            terms.append([])
-            for c in range(HALF // P):
-                terms[h].append(edge_tile(h * (HALF // P) + c))
-                if h == 0 and c > 0:
-                    owns.append(gather_state(states[c], c))
-            for r in range(PAGES):
-                place(h, r, terms[h])
-                if h == J // HALF - 1:
-                    nc.sync.dma_start(out[P * r : P * (r + 1), :], pages[r][:])
-        for r in range(PAGES, ROW_TILES):
-            for h in range(J // HALF):
-                place(h, r, terms[h])
-            nc.sync.dma_start(out[P * r : P * (r + 1), :], pages[r % PAGES][:])
+        first = []
+        for e in range(4):
+            first.append(edge_tile(e))
+            if e > 0:
+                owns.append(gather_state(states[e], e))
+        second = []
+        for r in range(ROW_TILES):
+            place(0, r, first)
+            if r < 2:
+                second.append(edge_tile(4 + 2 * r))
+                second.append(edge_tile(5 + 2 * r))
+        for r in range(ROW_TILES):
+            place(1, r, second)
+            nc.sync.dma_start(out[P * r : P * (r + 1), :], pages[r][:])

@@ -21,13 +21,20 @@ SIGMOID = mybir.ActivationFunctionType.Sigmoid
 
 P = 128
 PACK = 4
-PASSES = K // (P * PACK)
-QUADS = 4
+K_PASS = P * PACK
+PASSES = K // K_PASS
+QUAD = 32
+QUADS = P // QUAD
+LIVE = 4
+GROUP = 16
 EDGE_TILES = J // P
 ROW_TILES = N // P
 HALF = 512
-PAGES = 4
+TILES_A_HALF = HALF // P
 TGT, SRC = 0, 1
+
+GATED_TAG = {0: "state0", 2: "state1"}
+ETA_TAG = ("raw_o1", "eta1", "eta2", "eta3", "raw_o1", "eta2", "raw_o1", "eta2")
 
 
 def tile_list_rgg_ownL_kernel(
@@ -36,11 +43,11 @@ def tile_list_rgg_ownL_kernel(
     nc = tc.nc
     with ExitStack() as ctx:
         keep = ctx.enter_context(tc.tile_pool(name="keep", bufs=1))
-        ring = ctx.enter_context(tc.tile_pool(name="ring", bufs=2))
+        ring = ctx.enter_context(tc.tile_pool(name="ring", bufs=ROW_TILES))
         psum = ctx.enter_context(tc.psum_pool(name="psum", bufs=2))
 
-        tgt_list = keep.tile([P, J // 16], U16, name="tgt_list")
-        src_list = keep.tile([P, J // 16], U16, name="src_list")
+        tgt_list = keep.tile([P, J // GROUP], U16, name="tgt_list")
+        src_list = keep.tile([P, J // GROUP], U16, name="src_list")
         lists = (tgt_list, src_list)
         tab_s = keep.tile([P, T], U8, name="tab_s", align_bytes=64)
         tab_w = keep.tile([P, T], U32, name="tab_w", align_bytes=64)
@@ -53,41 +60,38 @@ def tile_list_rgg_ownL_kernel(
         wgo_rows = keep.tile([P, J], F32, name="wgo_rows")
         wgo_cols = keep.tile([P, EDGE_TILES], F32, name="wgo_cols")
         ident = keep.tile([P, P], F32, name="ident")
-        pages = [keep.tile([P, T], F32, name="page%d" % r) for r in range(PAGES)]
+        wgo_cut = keep.tile([P, P], F32, name="wgo_cut")
+        pages = [keep.tile([P, T], F32, name="page%d" % r) for r in range(ROW_TILES - 1)]
 
-        for plane in (tab_s, wa_s, wc_s, moved_s):
-            nc.gpsimd.memset(plane[:].bitcast(I32), 0)
+        nc.gpsimd.memset(tab_s[:].bitcast(I32), 0)
+        nc.gpsimd.memset(wgo_cut[:], 0.0)
         make_identity(nc, ident[:])
-        warm = keep.tile([P, 16], F32, name="warm")
-        nc.vector.memset(warm[:, 0:1], 0.0)
-        nc.scalar.activation(warm[:, 8:9], warm[:, 0:1], SIGMOID)
-        nc.vector.memset(pages[0][:].bitcast(I32), 0)
-        for page in pages[1:]:
-            nc.gpsimd.memset(page[:].bitcast(I32), 0)
+        for cleared in [wa_s, wc_s, moved_s] + pages:
+            nc.vector.memset(cleared[:].bitcast(I32), 0)
 
         nc.sync.dma_start(tgt_list[:], offs2)
         nc.sync.dma_start(src_list[:], offs)
         for q in range(QUADS):
             nc.sync.dma_start(
-                tab_s[:].bitcast(I32)[32 * q : 32 * q + 4 * PASSES, :],
-                tab_scales.bitcast(I32)[:, 4 * q : 4 * q + 4, :],
+                tab_s[:].bitcast(I32)[QUAD * q : QUAD * q + LIVE * PASSES, :],
+                tab_scales.bitcast(I32)[:, LIVE * q : LIVE * (q + 1), :],
             )
         nc.sync.dma_start(tab_w[:].bitcast(I32), tab_words[0].rearrange("p t b -> p (t b)").bitcast(I32))
 
-        def load_scales(plane, rows):
-            for q in range(QUADS):
+        def load_scales(plane, rows, quads):
+            for q in quads:
                 nc.sync.dma_start(
-                    plane[:].bitcast(I32)[32 * q : 32 * q + 4, :, :],
-                    rows.bitcast(I32)[:, 4 * q : 4 * q + 4, :].rearrange("a r w -> r a w"),
+                    plane[:].bitcast(I32)[QUAD * q : QUAD * q + LIVE, :, :],
+                    rows.bitcast(I32)[:, LIVE * q : LIVE * (q + 1), :].rearrange("a r w -> r a w"),
                 )
 
-        def load_raw(w, a):
-            raw = ring.tile([P, PACK, N], F32, name="raw", bufs=4)
-            nc.sync.dma_start(raw[:], w[512 * a : 512 * (a + 1), :].rearrange("(p i) n -> p i n", i=PACK))
+        def load_raw(w, a, name):
+            raw = keep.tile([P, PACK, N], F32, name="raw", tag="%s%d" % (name, a), align_bytes=64)
+            nc.sync.dma_start(raw[:], w[K_PASS * a : K_PASS * (a + 1), :].rearrange("(p i) n -> p i n", i=PACK))
             return raw
 
-        def weave(raw):
-            woven = ring.tile([P, N, PACK], BF16, name="woven", align_bytes=64, bufs=4)
+        def weave(raw, tag):
+            woven = keep.tile([P, N, PACK], BF16, name="woven", tag=tag, align_bytes=64)
             nc.scalar.copy(
                 woven[:].rearrange("p (c u) i -> p c i u", u=4),
                 raw[:].rearrange("p i (c u) -> p c i u", u=4),
@@ -103,57 +107,61 @@ def tile_list_rgg_ownL_kernel(
             return codes[:].bitcast(FP8X4), plane[:]
 
         def load_state(r):
-            state = ring.tile([P, T], F32, name="state", bufs=3)
+            state = keep.tile([P, T], F32, name="state", tag="state%d" % r, align_bytes=64)
             nc.sync.dma_start(state[:], rT[P * r : P * (r + 1), :])
             return state
 
-        def gather_state(state, r):
-            own = keep.tile([P, J], F32, name="own%d" % r)
+        def gather_state(state, tag):
+            own = keep.tile([P, J], F32, name="own", tag=tag, align_bytes=64)
             nc.vector.tensor_tensor(own[:], state[:].indirect(tgt_list[:]), wgo_rows[:], MULT)
             return own
 
-        raw_o = [load_raw(wo, a) for a in range(PASSES)]
-        raw_b = [load_raw(wb, 0)]
-        load_scales(wa_s, wa_scales)
+        raw_b = [load_raw(wb, a, "raw_b") for a in range(PASSES)]
         nc.sync.dma_start(wa_w[:].bitcast(I32), wa_words.rearrange("a p n b -> p a (n b)").bitcast(I32))
-        load_scales(wc_s, wc_scales)
+        load_scales(wa_s, wa_scales, (0, 1))
         nc.sync.dma_start(wc_w[:].bitcast(I32), wc_words.rearrange("a p m -> p a m").bitcast(I32))
-        raw_b.append(load_raw(wb, 1))
+        raw_o = [load_raw(wo, 0, "raw_o")]
+        load_scales(wa_s, wa_scales, (2, 3))
+        raw_o.append(load_raw(wo, 1, "raw_o"))
+        load_scales(wc_s, wc_scales, range(QUADS))
+        nc.sync.dma_start(wgo_cut[0:EDGE_TILES, :], wgo[0].rearrange("(e p) -> e p", p=P))
         nc.sync.dma_start(wgo_rows[:], wgo)
-        states = [load_state(r) for r in range(3)]
+        states = [load_state(r) for r in range(ROW_TILES)]
 
         for side in (TGT, SRC):
             nc.vector.tensor_copy(got_s[:, side * J : (side + 1) * J], tab_s[:].indirect(lists[side][:]))
-        nc.scalar.dma_start(moved_s[:].bitcast(I32)[0 : P - 4, :], got_s[:].bitcast(I32)[4:P, :])
-        parted = []
-        for side in (TGT, SRC):
-            got_w = ring.tile([P, J], U32, name="got_w", align_bytes=64)
+        span = QUAD * (QUADS - 1) + LIVE
+        nc.gpsimd.dma_start(moved_s[:].bitcast(I32)[0:span, :], got_s[:].bitcast(I32)[LIVE : LIVE + span, :])
+
+        def gather_words(side):
+            got_w = keep.tile([P, J], U32, name="got_w%d" % side, align_bytes=64)
             nc.vector.tensor_copy(got_w[:], tab_w[:].indirect(lists[side][:]))
             halves = keep.tile([P, PASSES, 2 * J], U8, name="parted%d" % side, align_bytes=64)
             nc.vector.tensor_copy(
                 halves[:].bitcast(U16), got_w[:].bitcast(U16).rearrange("p (j a) -> p a j", a=PASSES)
             )
-            parted.append(halves)
+            return halves
+
+        parted = [gather_words(side) for side in (TGT, SRC)]
 
         def nodes(side, a, e):
             codes = parted[side][:, a, 2 * P * e : 2 * P * (e + 1)].bitcast(FP4X4)
             plane = (got_s, moved_s)[a][:, side * J + P * e : side * J + P * (e + 1)]
             return codes, plane
 
-        wo_q = [quantise(weave(raw_o[a]), "wo%d" % a) for a in range(PASSES)]
-        wb_q = [quantise(weave(raw_b[a]), "wb%d" % a) for a in range(PASSES)]
+        wb_q = [quantise(weave(raw_b[a], "woven_b%d" % a), "wb%d" % a) for a in range(PASSES)]
+        wo_q = [quantise(weave(raw_o[a], "woven_o%d" % a), "wo%d" % a) for a in range(PASSES)]
+        last_page = keep.tile([P, T], F32, name="last_page", tag="raw_o0", align_bytes=64)
+        nc.vector.memset(last_page[:].bitcast(I32), 0)
+        pages.append(last_page)
         wa_q = [(wa_w[:, a, :].bitcast(FP8X4), wa_s[:, a, :]) for a in range(PASSES)]
         wc_q = [(wc_w[:, a, :].bitcast(FP4X4), wc_s[:, a, :]) for a in range(PASSES)]
 
-        for h in range(J // HALF):
-            turned = psum.tile([P, HALF], F32, name="sums")
-            for c in range(HALF // P):
-                e = h * (HALF // P) + c
-                nc.tensor.transpose(turned[:, P * c : P * (c + 1)], wgo_rows[:, P * e : P * (e + 1)], ident[:])
-            nc.scalar.copy(wgo_cols[:, 4 * h : 4 * h + 4], turned[:, 0:HALF:P])
+        turned = psum.tile([P, HALF], F32, name="sums")
+        nc.tensor.transpose(turned[:, 0:P], wgo_cut[:], ident[:])
+        nc.scalar.copy(wgo_cols[:], turned[:, 0:EDGE_TILES])
 
-        owns = [gather_state(states[0], 0)]
-        states.append(load_state(3))
+        owns = [gather_state(states[0], "woven_o1")]
 
         def product(bank, terms, e):
             steps = [(side, w, a) for side, w in terms for a in range(PASSES)]
@@ -171,41 +179,43 @@ def tile_list_rgg_ownL_kernel(
             product(ms, ((SRC, wc_q),), e)
             ow = psum.tile([P, N], F32, name="ow")
             product(ow, ((TGT, wo_q),), e)
-            eta = ring.tile([P, N], F32, name="eta")
+            eta = keep.tile([P, N], F32, name="eta", tag=ETA_TAG[e], align_bytes=64)
             nc.scalar.activation(eta[:], za[:], SIGMOID)
             kept = keep.tile([P, N], F32, name="kept%d" % e)
             nc.scalar.activation(kept[:], ow[:], COPY, scale=wgo_cols[:, e : e + 1])
-            gated = keep.tile([P, N], F32, name="gated%d" % e)
+            gated = keep.tile([P, N], F32, name="gated", tag=GATED_TAG.get(e, "gated%d" % e), align_bytes=64)
             nc.vector.scalar_tensor_tensor(gated[:], ms[:], wgo_cols[:, e : e + 1], eta[:], MULT, MULT)
             return kept, gated
 
         def place(h, r, terms):
             sums = psum.tile([P, HALF], F32, name="sums")
-            for c in range(HALF // P):
+            for c in range(TILES_A_HALF):
                 for s, term in enumerate(terms[c]):
                     nc.tensor.matmul(
                         sums[:, P * c : P * (c + 1)], term[:, P * r : P * (r + 1)], ident[:],
                         start=(s == 0), stop=(s == 1), is_transpose=True,
                     )
-            update = ring.tile([P, HALF], F32, name="update", bufs=4)
+            update = ring.tile([P, HALF], F32, name="update")
             nc.scalar.copy(update[:], sums[:])
-            cols = HALF // 16
+            cols = HALF // GROUP
             nc.vector.tensor_tensor(
-                pages[r % PAGES][:].indirect(tgt_list[:, cols * h : cols * (h + 1)]),
+                pages[r][:].indirect(tgt_list[:, cols * h : cols * (h + 1)]),
                 update[:], owns[r][:, HALF * h : HALF * (h + 1)], ADD,
             )
 
         first = []
-        for e in range(4):
+        for e in range(TILES_A_HALF):
             first.append(edge_tile(e))
-            if e > 0:
-                owns.append(gather_state(states[e], e))
+            if e % 2 == 1:
+                owns.append(gather_state(states[len(owns)], ETA_TAG[e]))
+        owns.append(gather_state(states[ROW_TILES - 1], "state2"))
+
         second = []
-        for r in range(ROW_TILES):
-            place(0, r, first)
-            if r < 2:
-                second.append(edge_tile(4 + 2 * r))
-                second.append(edge_tile(5 + 2 * r))
+        for step in range(ROW_TILES):
+            place(0, ROW_TILES - 1 - step, first)
+            if step < TILES_A_HALF // 2:
+                second.append(edge_tile(TILES_A_HALF + 2 * step))
+                second.append(edge_tile(TILES_A_HALF + 2 * step + 1))
         for r in range(ROW_TILES):
             place(1, r, second)
             nc.sync.dma_start(out[P * r : P * (r + 1), :], pages[r][:])

@@ -33,8 +33,9 @@ HALF = 512
 TILES_A_HALF = HALF // P
 TGT, SRC = 0, 1
 
-GATED_TAG = {0: "state0", 2: "state1"}
-ETA_TAG = ("raw_o1", "eta1", "eta2", "eta3", "raw_o1", "eta2", "raw_o1", "eta2")
+BANKS = 8
+PAIR = 2
+GATED_TAGS = ("state1", "state2", "raw_o1", "tab_w")
 
 
 def tile_list_rgg_ownL_kernel(
@@ -44,13 +45,18 @@ def tile_list_rgg_ownL_kernel(
     with ExitStack() as ctx:
         keep = ctx.enter_context(tc.tile_pool(name="keep", bufs=1))
         ring = ctx.enter_context(tc.tile_pool(name="ring", bufs=ROW_TILES))
-        psum = ctx.enter_context(tc.psum_pool(name="psum", bufs=2))
+        psum = ctx.enter_context(tc.psum_pool(name="psum", bufs=1))
+        taken = []
+
+        def bank(again=False):
+            taken.append(taken[-1] if again else (taken[-1] + 1) % BANKS if taken else 0)
+            return psum.tile([P, HALF], F32, name="bank", tag="bank%d" % taken[-1])
 
         tgt_list = keep.tile([P, J // GROUP], U16, name="tgt_list")
         src_list = keep.tile([P, J // GROUP], U16, name="src_list")
         lists = (tgt_list, src_list)
-        tab_s = keep.tile([P, T], U8, name="tab_s", align_bytes=64)
-        tab_w = keep.tile([P, T], U32, name="tab_w", align_bytes=64)
+        tab_s = keep.tile([P, T], U8, name="tab_s", tag="got_w%d" % SRC, align_bytes=64)
+        tab_w = keep.tile([P, T], U32, name="tab_w", tag="tab_w", align_bytes=64)
         got_s = keep.tile([P, 2 * J], U8, name="got_s", align_bytes=64)
         moved_s = keep.tile([P, 2 * J], U8, name="moved_s", align_bytes=64)
         wa_w = keep.tile([P, PASSES, N], U32, name="wa_w", align_bytes=64)
@@ -61,7 +67,7 @@ def tile_list_rgg_ownL_kernel(
         wgo_cols = keep.tile([P, EDGE_TILES], F32, name="wgo_cols")
         ident = keep.tile([P, P], F32, name="ident")
         wgo_cut = keep.tile([P, P], F32, name="wgo_cut")
-        pages = [keep.tile([P, T], F32, name="page%d" % r) for r in range(ROW_TILES - 1)]
+        pages = [keep.tile([P, T], F32, name="page%d" % r) for r in range(ROW_TILES // 2)]
 
         nc.gpsimd.memset(tab_s[:].bitcast(I32), 0)
         nc.gpsimd.memset(wgo_cut[:], 0.0)
@@ -76,6 +82,7 @@ def tile_list_rgg_ownL_kernel(
                 tab_s[:].bitcast(I32)[QUAD * q : QUAD * q + LIVE * PASSES, :],
                 tab_scales.bitcast(I32)[:, LIVE * q : LIVE * (q + 1), :],
             )
+
         nc.sync.dma_start(tab_w[:].bitcast(I32), tab_words[0].rearrange("p t b -> p (t b)").bitcast(I32))
 
         def load_scales(plane, rows, quads):
@@ -116,33 +123,36 @@ def tile_list_rgg_ownL_kernel(
             nc.vector.tensor_tensor(own[:], state[:].indirect(tgt_list[:]), wgo_rows[:], MULT)
             return own
 
-        raw_b = [load_raw(wb, a, "raw_b") for a in range(PASSES)]
-        nc.sync.dma_start(wa_w[:].bitcast(I32), wa_words.rearrange("a p n b -> p a (n b)").bitcast(I32))
-        load_scales(wa_s, wa_scales, (0, 1))
-        nc.sync.dma_start(wc_w[:].bitcast(I32), wc_words.rearrange("a p m -> p a m").bitcast(I32))
-        raw_o = [load_raw(wo, 0, "raw_o")]
-        load_scales(wa_s, wa_scales, (2, 3))
-        raw_o.append(load_raw(wo, 1, "raw_o"))
-        load_scales(wc_s, wc_scales, range(QUADS))
-        nc.sync.dma_start(wgo_cut[0:EDGE_TILES, :], wgo[0].rearrange("(e p) -> e p", p=P))
-        nc.sync.dma_start(wgo_rows[:], wgo)
-        states = [load_state(r) for r in range(ROW_TILES)]
-
-        for side in (TGT, SRC):
+        def gather_scales(side):
             nc.vector.tensor_copy(got_s[:, side * J : (side + 1) * J], tab_s[:].indirect(lists[side][:]))
-        span = QUAD * (QUADS - 1) + LIVE
-        nc.gpsimd.dma_start(moved_s[:].bitcast(I32)[0:span, :], got_s[:].bitcast(I32)[LIVE : LIVE + span, :])
 
         def gather_words(side):
-            got_w = keep.tile([P, J], U32, name="got_w%d" % side, align_bytes=64)
+            got_w = keep.tile([P, J], U32, name="got_w", tag="got_w%d" % side, align_bytes=64)
             nc.vector.tensor_copy(got_w[:], tab_w[:].indirect(lists[side][:]))
+            return got_w
+
+        def part(got_w, side):
             halves = keep.tile([P, PASSES, 2 * J], U8, name="parted%d" % side, align_bytes=64)
             nc.vector.tensor_copy(
                 halves[:].bitcast(U16), got_w[:].bitcast(U16).rearrange("p (j a) -> p a j", a=PASSES)
             )
             return halves
 
-        parted = [gather_words(side) for side in (TGT, SRC)]
+        got_tgt = gather_words(TGT)
+        gather_scales(TGT)
+        gather_scales(SRC)
+        parted = [part(got_tgt, TGT), part(gather_words(SRC), SRC)]
+
+        raw_b = [load_raw(wb, a, "raw_b") for a in range(PASSES)]
+        nc.sync.dma_start(wgo_cut[0:EDGE_TILES, :], wgo[0].rearrange("(e p) -> e p", p=P))
+        nc.sync.dma_start(wa_w[:].bitcast(I32), wa_words.rearrange("a p n b -> p a (n b)").bitcast(I32))
+        nc.sync.dma_start(wc_w[:].bitcast(I32), wc_words.rearrange("a p m -> p a m").bitcast(I32))
+        load_scales(wa_s, wa_scales, range(QUADS))
+        raw_o = [load_raw(wo, a, "raw_o") for a in range(PASSES)]
+        load_scales(wc_s, wc_scales, range(QUADS))
+        span = 112
+        nc.sync.dma_start(moved_s[:].bitcast(I32)[0:span, :], got_s[:].bitcast(I32)[LIVE : LIVE + span, :])
+        states = [load_state(r) for r in range(ROW_TILES)]
 
         def nodes(side, a, e):
             codes = parted[side][:, a, 2 * P * e : 2 * P * (e + 1)].bitcast(FP4X4)
@@ -151,46 +161,57 @@ def tile_list_rgg_ownL_kernel(
 
         wb_q = [quantise(weave(raw_b[a], "woven_b%d" % a), "wb%d" % a) for a in range(PASSES)]
         wo_q = [quantise(weave(raw_o[a], "woven_o%d" % a), "wo%d" % a) for a in range(PASSES)]
-        last_page = keep.tile([P, T], F32, name="last_page", tag="raw_o0", align_bytes=64)
-        nc.vector.memset(last_page[:].bitcast(I32), 0)
-        pages.append(last_page)
         wa_q = [(wa_w[:, a, :].bitcast(FP8X4), wa_s[:, a, :]) for a in range(PASSES)]
         wc_q = [(wc_w[:, a, :].bitcast(FP4X4), wc_s[:, a, :]) for a in range(PASSES)]
 
-        turned = psum.tile([P, HALF], F32, name="sums")
+        turned = bank()
         nc.tensor.transpose(turned[:, 0:P], wgo_cut[:], ident[:])
         nc.scalar.copy(wgo_cols[:], turned[:, 0:EDGE_TILES])
+        for h in range(J // HALF):
+            spread = bank()
+            for c in range(TILES_A_HALF):
+                e = TILES_A_HALF * h + c
+                nc.tensor.transpose(spread[:, P * c : P * (c + 1)], wgo_cols[:, e : e + 1].to_broadcast([P, P]), ident[:])
+            nc.scalar.copy(wgo_rows[:, HALF * h : HALF * (h + 1)], spread[:])
 
-        owns = [gather_state(states[0], "woven_o1")]
+        def late_page(tag):
+            page = keep.tile([P, T], F32, name="late_page", tag=tag, align_bytes=64)
+            nc.gpsimd.memset(page[:].bitcast(I32), 0)
+            pages.append(page)
 
-        def product(bank, terms, e):
+        def product(terms, e):
+            sums = bank()
             steps = [(side, w, a) for side, w in terms for a in range(PASSES)]
             for s, (side, w, a) in enumerate(steps):
                 codes, plane = nodes(side, a, e)
                 nc.tensor.matmul_mx(
-                    out=bank[:], lhsT=codes, lhsT_scale=plane, rhs=w[a][0], rhs_scale=w[a][1],
+                    out=sums[:], lhsT=codes, lhsT_scale=plane, rhs=w[a][0], rhs_scale=w[a][1],
                     start=(s == 0), stop=(s == len(steps) - 1),
                 )
+            return sums
 
-        def edge_tile(e):
-            za = psum.tile([P, N], F32, name="za")
-            product(za, ((TGT, wa_q), (SRC, wb_q)), e)
-            ms = psum.tile([P, N], F32, name="ms")
-            product(ms, ((SRC, wc_q),), e)
-            ow = psum.tile([P, N], F32, name="ow")
-            product(ow, ((TGT, wo_q),), e)
-            eta = keep.tile([P, N], F32, name="eta", tag=ETA_TAG[e], align_bytes=64)
-            nc.scalar.activation(eta[:], za[:], SIGMOID)
+        def messages(pair):
+            eta = keep.tile([P, PAIR, N], F32, name="eta", tag="eta%d" % pair, align_bytes=64)
+            sent = keep.tile([P, PAIR, N], F32, name="sent%d" % pair)
+            for c in range(PAIR):
+                e = PAIR * pair + c
+                nc.scalar.activation(eta[:, c, :], product(((TGT, wa_q), (SRC, wb_q)), e)[:], SIGMOID)
+                nc.scalar.activation(
+                    sent[:, c, :], product(((SRC, wc_q),), e)[:], COPY, scale=wgo_cols[:, e : e + 1]
+                )
+            gated = keep.tile([P, PAIR, N], F32, name="gated", tag=GATED_TAGS[pair], align_bytes=64)
+            nc.vector.tensor_tensor(gated[:], sent[:], eta[:], MULT)
+            return [gated[:, c, :] for c in range(PAIR)]
+
+        def projection(e):
             kept = keep.tile([P, N], F32, name="kept%d" % e)
-            nc.scalar.activation(kept[:], ow[:], COPY, scale=wgo_cols[:, e : e + 1])
-            gated = keep.tile([P, N], F32, name="gated", tag=GATED_TAG.get(e, "gated%d" % e), align_bytes=64)
-            nc.vector.scalar_tensor_tensor(gated[:], ms[:], wgo_cols[:, e : e + 1], eta[:], MULT, MULT)
-            return kept, gated
+            nc.scalar.activation(kept[:], product(((TGT, wo_q),), e)[:], COPY, scale=wgo_cols[:, e : e + 1])
+            return kept[:]
 
-        def place(h, r, terms):
-            sums = psum.tile([P, HALF], F32, name="sums")
+        def place(h, r, gated, kept, again=False):
+            sums = bank(again)
             for c in range(TILES_A_HALF):
-                for s, term in enumerate(terms[c]):
+                for s, term in enumerate((gated[c], kept[c])):
                     nc.tensor.matmul(
                         sums[:, P * c : P * (c + 1)], term[:, P * r : P * (r + 1)], ident[:],
                         start=(s == 0), stop=(s == 1), is_transpose=True,
@@ -203,19 +224,22 @@ def tile_list_rgg_ownL_kernel(
                 update[:], owns[r][:, HALF * h : HALF * (h + 1)], ADD,
             )
 
-        first = []
-        for e in range(TILES_A_HALF):
-            first.append(edge_tile(e))
-            if e % 2 == 1:
-                owns.append(gather_state(states[len(owns)], ETA_TAG[e]))
-        owns.append(gather_state(states[ROW_TILES - 1], "state2"))
-
-        second = []
-        for step in range(ROW_TILES):
-            place(0, ROW_TILES - 1 - step, first)
-            if step < TILES_A_HALF // 2:
-                second.append(edge_tile(TILES_A_HALF + 2 * step))
-                second.append(edge_tile(TILES_A_HALF + 2 * step + 1))
+        late_page("woven_o1")
+        owns = [gather_state(states[0], "own0")]
+        late_page("state0")
+        owns.append(gather_state(states[1], "own1"))
+        gated_a = messages(0)
+        owns.append(gather_state(states[2], "own2"))
+        gated_a = gated_a + messages(1)
+        owns.append(gather_state(states[3], "eta1"))
+        kept_a = [projection(e) for e in range(TILES_A_HALF)]
+        place(0, 0, gated_a, kept_a)
+        place(0, 1, gated_a, kept_a)
+        gated_b = messages(2)
+        place(0, 2, gated_a, kept_a, again=True)
+        gated_b = gated_b + messages(3)
+        place(0, 3, gated_a, kept_a, again=True)
+        kept_b = [projection(e) for e in range(TILES_A_HALF, EDGE_TILES)]
         for r in range(ROW_TILES):
-            place(1, r, second)
+            place(1, r, gated_b, kept_b)
             nc.sync.dma_start(out[P * r : P * (r + 1), :], pages[r][:])

@@ -35,7 +35,8 @@ TGT, SRC = 0, 1
 
 BANKS = 8
 PAIR = 2
-GATED_TAGS = ("state1", "state2", "raw_o1", "tab_w")
+GATED_TAGS = ("raw_b0", "raw_b1", "raw_o0", "raw_o1")
+SPARE = QUAD - LIVE * PASSES
 
 
 def tile_list_rgg_ownL_kernel(
@@ -44,21 +45,18 @@ def tile_list_rgg_ownL_kernel(
     nc = tc.nc
     with ExitStack() as ctx:
         keep = ctx.enter_context(tc.tile_pool(name="keep", bufs=1))
-        ring = ctx.enter_context(tc.tile_pool(name="ring", bufs=ROW_TILES))
         psum = ctx.enter_context(tc.psum_pool(name="psum", bufs=1))
-        taken = []
 
-        def bank(again=False):
-            taken.append(taken[-1] if again else (taken[-1] + 1) % BANKS if taken else 0)
-            return psum.tile([P, HALF], F32, name="bank", tag="bank%d" % taken[-1])
+        def bank(b):
+            return psum.tile([P, HALF], F32, name="bank", tag="bank%d" % b)
 
         tgt_list = keep.tile([P, J // GROUP], U16, name="tgt_list")
         src_list = keep.tile([P, J // GROUP], U16, name="src_list")
         lists = (tgt_list, src_list)
-        tab_s = keep.tile([P, T], U8, name="tab_s", tag="got_w%d" % SRC, align_bytes=64)
+        tab_s = keep.tile([P, T], U8, name="tab_s", align_bytes=64)
         tab_w = keep.tile([P, T], U32, name="tab_w", tag="tab_w", align_bytes=64)
         got_s = keep.tile([P, 2 * J], U8, name="got_s", align_bytes=64)
-        moved_s = keep.tile([P, 2 * J], U8, name="moved_s", align_bytes=64)
+        planes = [keep.tile([P, 2 * J], U8, name="plane%d" % a, align_bytes=64) for a in range(PASSES)]
         wa_w = keep.tile([P, PASSES, N], U32, name="wa_w", align_bytes=64)
         wc_w = keep.tile([P, PASSES, 2 * N], U8, name="wc_w", align_bytes=64)
         wa_s = keep.tile([P, PASSES, N], U8, name="wa_s", align_bytes=64)
@@ -67,23 +65,25 @@ def tile_list_rgg_ownL_kernel(
         wgo_cols = keep.tile([P, EDGE_TILES], F32, name="wgo_cols")
         ident = keep.tile([P, P], F32, name="ident")
         wgo_cut = keep.tile([P, P], F32, name="wgo_cut")
-        pages = [keep.tile([P, T], F32, name="page%d" % r) for r in range(ROW_TILES // 2)]
 
-        nc.gpsimd.memset(tab_s[:].bitcast(I32), 0)
+        warm = keep.tile([P, 16], F32, name="warm")
+        nc.gpsimd.memset(warm[:, 0:8], 0.0)
+        nc.scalar.activation(warm[:, 8:9], warm[:, 0:1], SIGMOID)
+
+        for q in range(QUADS):
+            nc.vector.memset(tab_s[:].bitcast(I32)[QUAD * q : QUAD * q + SPARE, :], 0)
         nc.gpsimd.memset(wgo_cut[:], 0.0)
         make_identity(nc, ident[:])
-        for cleared in [wa_s, wc_s, moved_s] + pages:
+        for cleared in planes + [wa_s, wc_s]:
             nc.vector.memset(cleared[:].bitcast(I32), 0)
 
         nc.sync.dma_start(tgt_list[:], offs2)
-        nc.sync.dma_start(src_list[:], offs)
         for q in range(QUADS):
             nc.sync.dma_start(
-                tab_s[:].bitcast(I32)[QUAD * q : QUAD * q + LIVE * PASSES, :],
+                tab_s[:].bitcast(I32)[QUAD * q + SPARE : QUAD * (q + 1), :],
                 tab_scales.bitcast(I32)[:, LIVE * q : LIVE * (q + 1), :],
             )
-
-        nc.sync.dma_start(tab_w[:].bitcast(I32), tab_words[0].rearrange("p t b -> p (t b)").bitcast(I32))
+        nc.sync.dma_start(src_list[:], offs)
 
         def load_scales(plane, rows, quads):
             for q in quads:
@@ -138,25 +138,29 @@ def tile_list_rgg_ownL_kernel(
             )
             return halves
 
-        got_tgt = gather_words(TGT)
+        raw_b = [load_raw(wb, 0, "raw_b")]
+        nc.sync.dma_start(wgo_cut[0:EDGE_TILES, :], wgo[0].rearrange("(e p) -> e p", p=P))
+        nc.sync.dma_start(tab_w[:].bitcast(I32), tab_words[0].rearrange("p t b -> p (t b)").bitcast(I32))
         gather_scales(TGT)
         gather_scales(SRC)
-        parted = [part(got_tgt, TGT), part(gather_words(SRC), SRC)]
+        got = [gather_words(side) for side in (TGT, SRC)]
+        parted = [part(got[side], side) for side in (TGT, SRC)]
 
-        raw_b = [load_raw(wb, a, "raw_b") for a in range(PASSES)]
-        nc.sync.dma_start(wgo_cut[0:EDGE_TILES, :], wgo[0].rearrange("(e p) -> e p", p=P))
+        raw_b.append(load_raw(wb, 1, "raw_b"))
+        raw_o = [load_raw(wo, a, "raw_o") for a in range(PASSES)]
+        for a in range(PASSES):
+            down = SPARE + LIVE * a
+            nc.sync.dma_start(planes[a][:].bitcast(I32)[0 : P - down, :], got_s[:].bitcast(I32)[down:P, :])
+        load_scales(wa_s, wa_scales, range(QUADS))
+        states = [load_state(r) for r in range(2)]
+        load_scales(wc_s, wc_scales, range(QUADS))
         nc.sync.dma_start(wa_w[:].bitcast(I32), wa_words.rearrange("a p n b -> p a (n b)").bitcast(I32))
         nc.sync.dma_start(wc_w[:].bitcast(I32), wc_words.rearrange("a p m -> p a m").bitcast(I32))
-        load_scales(wa_s, wa_scales, range(QUADS))
-        raw_o = [load_raw(wo, a, "raw_o") for a in range(PASSES)]
-        load_scales(wc_s, wc_scales, range(QUADS))
-        span = 112
-        nc.sync.dma_start(moved_s[:].bitcast(I32)[0:span, :], got_s[:].bitcast(I32)[LIVE : LIVE + span, :])
-        states = [load_state(r) for r in range(ROW_TILES)]
+        states = states + [load_state(r) for r in range(2, ROW_TILES)]
 
         def nodes(side, a, e):
             codes = parted[side][:, a, 2 * P * e : 2 * P * (e + 1)].bitcast(FP4X4)
-            plane = (got_s, moved_s)[a][:, side * J + P * e : side * J + P * (e + 1)]
+            plane = planes[a][:, side * J + P * e : side * J + P * (e + 1)]
             return codes, plane
 
         wb_q = [quantise(weave(raw_b[a], "woven_b%d" % a), "wb%d" % a) for a in range(PASSES)]
@@ -164,82 +168,97 @@ def tile_list_rgg_ownL_kernel(
         wa_q = [(wa_w[:, a, :].bitcast(FP8X4), wa_s[:, a, :]) for a in range(PASSES)]
         wc_q = [(wc_w[:, a, :].bitcast(FP4X4), wc_s[:, a, :]) for a in range(PASSES)]
 
-        turned = bank()
+        turned = bank(BANKS - 1)
         nc.tensor.transpose(turned[:, 0:P], wgo_cut[:], ident[:])
         nc.scalar.copy(wgo_cols[:], turned[:, 0:EDGE_TILES])
         for h in range(J // HALF):
-            spread = bank()
+            spread = bank(BANKS - 2 - h)
             for c in range(TILES_A_HALF):
                 e = TILES_A_HALF * h + c
                 nc.tensor.transpose(spread[:, P * c : P * (c + 1)], wgo_cols[:, e : e + 1].to_broadcast([P, P]), ident[:])
             nc.scalar.copy(wgo_rows[:, HALF * h : HALF * (h + 1)], spread[:])
 
-        def late_page(tag):
-            page = keep.tile([P, T], F32, name="late_page", tag=tag, align_bytes=64)
-            nc.gpsimd.memset(page[:].bitcast(I32), 0)
-            pages.append(page)
-
-        def product(terms, e):
-            sums = bank()
-            steps = [(side, w, a) for side, w in terms for a in range(PASSES)]
-            for s, (side, w, a) in enumerate(steps):
+        def passes(sums, side, w, e, steps, start, stop):
+            for a in steps:
                 codes, plane = nodes(side, a, e)
                 nc.tensor.matmul_mx(
                     out=sums[:], lhsT=codes, lhsT_scale=plane, rhs=w[a][0], rhs_scale=w[a][1],
-                    start=(s == 0), stop=(s == len(steps) - 1),
+                    start=start and a == 0, stop=stop and a == PASSES - 1,
                 )
-            return sums
 
-        def messages(pair):
+        def weighted(target, side, w, e, b):
+            sums = bank(b)
+            passes(sums, side, w, e, range(PASSES), True, True)
+            nc.scalar.activation(target, sums[:], COPY, scale=wgo_cols[:, e : e + 1])
+
+        def open_gate(e):
+            za = bank(e % TILES_A_HALF)
+            passes(za, SRC, wb_q, e, range(PASSES), True, False)
+            return za
+
+        def messages(pair, za, banks):
             eta = keep.tile([P, PAIR, N], F32, name="eta", tag="eta%d" % pair, align_bytes=64)
             sent = keep.tile([P, PAIR, N], F32, name="sent%d" % pair)
             for c in range(PAIR):
-                e = PAIR * pair + c
-                nc.scalar.activation(eta[:, c, :], product(((TGT, wa_q), (SRC, wb_q)), e)[:], SIGMOID)
-                nc.scalar.activation(
-                    sent[:, c, :], product(((SRC, wc_q),), e)[:], COPY, scale=wgo_cols[:, e : e + 1]
-                )
+                passes(za[c], TGT, wa_q, PAIR * pair + c, range(PASSES), False, True)
+                nc.scalar.activation(eta[:, c, :], za[c][:], SIGMOID)
+            for c in range(PAIR):
+                weighted(sent[:, c, :], SRC, wc_q, PAIR * pair + c, banks[c])
             gated = keep.tile([P, PAIR, N], F32, name="gated", tag=GATED_TAGS[pair], align_bytes=64)
             nc.vector.tensor_tensor(gated[:], sent[:], eta[:], MULT)
             return [gated[:, c, :] for c in range(PAIR)]
 
         def projection(e):
             kept = keep.tile([P, N], F32, name="kept%d" % e)
-            nc.scalar.activation(kept[:], product(((TGT, wo_q),), e)[:], COPY, scale=wgo_cols[:, e : e + 1])
+            weighted(kept[:], TGT, wo_q, e, TILES_A_HALF + e % TILES_A_HALF)
             return kept[:]
 
-        def place(h, r, gated, kept, again=False):
-            sums = bank(again)
+        def turn(target, h, r, b):
+            sums = bank(b)
             for c in range(TILES_A_HALF):
-                for s, term in enumerate((gated[c], kept[c])):
+                e = TILES_A_HALF * h + c
+                for s, term in enumerate((gated[e], kept[e])):
                     nc.tensor.matmul(
                         sums[:, P * c : P * (c + 1)], term[:, P * r : P * (r + 1)], ident[:],
                         start=(s == 0), stop=(s == 1), is_transpose=True,
                     )
-            update = ring.tile([P, HALF], F32, name="update")
-            nc.scalar.copy(update[:], sums[:])
-            cols = HALF // GROUP
+            nc.scalar.copy(target, sums[:])
+
+        def place(r, halves, banks):
+            update = keep.tile([P, HALF * len(halves)], F32, name="update%d_%d" % (r, halves[0]))
+            for i, h in enumerate(halves):
+                turn(update[:, HALF * i : HALF * (i + 1)], h, r, banks[i])
+            lo, hi = HALF * halves[0], HALF * (halves[-1] + 1)
             nc.vector.tensor_tensor(
-                pages[r][:].indirect(tgt_list[:, cols * h : cols * (h + 1)]),
-                update[:], owns[r][:, HALF * h : HALF * (h + 1)], ADD,
+                pages[r][:].indirect(tgt_list[:, lo // GROUP : hi // GROUP]), update[:], owns[r][:, lo:hi], ADD
             )
 
-        late_page("woven_o1")
-        owns = [gather_state(states[0], "own0")]
-        late_page("state0")
-        owns.append(gather_state(states[1], "own1"))
-        gated_a = messages(0)
-        owns.append(gather_state(states[2], "own2"))
-        gated_a = gated_a + messages(1)
-        owns.append(gather_state(states[3], "eta1"))
-        kept_a = [projection(e) for e in range(TILES_A_HALF)]
-        place(0, 0, gated_a, kept_a)
-        place(0, 1, gated_a, kept_a)
-        gated_b = messages(2)
-        place(0, 2, gated_a, kept_a, again=True)
-        gated_b = gated_b + messages(3)
-        place(0, 3, gated_a, kept_a, again=True)
-        kept_b = [projection(e) for e in range(TILES_A_HALF, EDGE_TILES)]
-        for r in range(ROW_TILES):
-            place(1, r, gated_b, kept_b)
+        def store(r):
             nc.sync.dma_start(out[P * r : P * (r + 1), :], pages[r][:])
+
+        owns, pages = [], []
+
+        def take_state(tag):
+            r = len(owns)
+            owns.append(gather_state(states[r], tag))
+            page = keep.tile([P, T], F32, name="page", tag="state%d" % r, align_bytes=64)
+            nc.gpsimd.memset(page[:].bitcast(I32), 0)
+            pages.append(page)
+
+        za = [open_gate(e) for e in range(4)]
+        kept = [projection(e) for e in range(4)]
+        take_state("woven_o1")
+        take_state("own1")
+        take_state("own2")
+        gated = messages(0, za[0:2], (4, 5)) + messages(1, za[2:4], (6, 7))
+        take_state("eta1")
+        place(0, [0], [4])
+        place(1, [0], [5])
+        gated = gated + messages(2, [open_gate(4), open_gate(5)], (0, 1))
+        place(2, [0], [1])
+        gated = gated + messages(3, [open_gate(6), open_gate(7)], (2, 3))
+        place(3, [0], [3])
+        kept = kept + [projection(e) for e in range(4, 8)]
+        for r in range(ROW_TILES):
+            place(r, [1], [r])
+            store(r)

@@ -36,7 +36,7 @@ TGT, SRC = 0, 1
 BANKS = 8
 PAIR = 2
 GATED_TAGS = ("raw_b0", "raw_b1", "raw_o0", "raw_o1")
-SPARE = QUAD - LIVE * PASSES
+APART = 16
 
 
 def tile_list_rgg_ownL_kernel(
@@ -53,10 +53,10 @@ def tile_list_rgg_ownL_kernel(
         tgt_list = keep.tile([P, J // GROUP], U16, name="tgt_list")
         src_list = keep.tile([P, J // GROUP], U16, name="src_list")
         lists = (tgt_list, src_list)
-        tab_s = keep.tile([P, T], U8, name="tab_s", align_bytes=64)
+        tab_s = keep.tile([P, T], U8, name="tab_s", tag="got_w%d" % SRC, align_bytes=64)
         tab_w = keep.tile([P, T], U32, name="tab_w", tag="tab_w", align_bytes=64)
         got_s = keep.tile([P, 2 * J], U8, name="got_s", align_bytes=64)
-        planes = [keep.tile([P, 2 * J], U8, name="plane%d" % a, align_bytes=64) for a in range(PASSES)]
+        moved_s = keep.tile([P, 2 * J], U8, name="moved_s", align_bytes=64)
         wa_w = keep.tile([P, PASSES, N], U32, name="wa_w", align_bytes=64)
         wc_w = keep.tile([P, PASSES, 2 * N], U8, name="wc_w", align_bytes=64)
         wa_s = keep.tile([P, PASSES, N], U8, name="wa_s", align_bytes=64)
@@ -66,24 +66,23 @@ def tile_list_rgg_ownL_kernel(
         ident = keep.tile([P, P], F32, name="ident")
         wgo_cut = keep.tile([P, P], F32, name="wgo_cut")
 
+        nc.gpsimd.memset(tab_s[:].bitcast(I32), 0)
         warm = keep.tile([P, 16], F32, name="warm")
         nc.gpsimd.memset(warm[:, 0:8], 0.0)
         nc.scalar.activation(warm[:, 8:9], warm[:, 0:1], SIGMOID)
 
-        for q in range(QUADS):
-            nc.vector.memset(tab_s[:].bitcast(I32)[QUAD * q : QUAD * q + SPARE, :], 0)
         nc.gpsimd.memset(wgo_cut[:], 0.0)
         make_identity(nc, ident[:])
-        for cleared in planes + [wa_s, wc_s]:
+        for cleared in [wa_s, wc_s, moved_s]:
             nc.vector.memset(cleared[:].bitcast(I32), 0)
 
         nc.sync.dma_start(tgt_list[:], offs2)
-        for q in range(QUADS):
-            nc.sync.dma_start(
-                tab_s[:].bitcast(I32)[QUAD * q + SPARE : QUAD * (q + 1), :],
-                tab_scales.bitcast(I32)[:, LIVE * q : LIVE * (q + 1), :],
-            )
         nc.sync.dma_start(src_list[:], offs)
+        for r in range(LIVE):
+            nc.sync.dma_start(
+                tab_s[:].bitcast(I32)[r:P:APART, :],
+                tab_scales.bitcast(I32).rearrange("a (q r) w -> r q a w", r=LIVE)[r],
+            )
 
         def load_scales(plane, rows, quads):
             for q in quads:
@@ -138,21 +137,20 @@ def tile_list_rgg_ownL_kernel(
             )
             return halves
 
-        raw_b = [load_raw(wb, 0, "raw_b")]
-        nc.sync.dma_start(wgo_cut[0:EDGE_TILES, :], wgo[0].rearrange("(e p) -> e p", p=P))
         nc.sync.dma_start(tab_w[:].bitcast(I32), tab_words[0].rearrange("p t b -> p (t b)").bitcast(I32))
+        nc.sync.dma_start(wgo_cut[0:EDGE_TILES, :], wgo[0].rearrange("(e p) -> e p", p=P))
+        got = [gather_words(TGT)]
         gather_scales(TGT)
         gather_scales(SRC)
-        got = [gather_words(side) for side in (TGT, SRC)]
+        got.append(gather_words(SRC))
         parted = [part(got[side], side) for side in (TGT, SRC)]
 
-        raw_b.append(load_raw(wb, 1, "raw_b"))
+        raw_b = [load_raw(wb, a, "raw_b") for a in range(PASSES)]
         raw_o = [load_raw(wo, a, "raw_o") for a in range(PASSES)]
-        for a in range(PASSES):
-            down = SPARE + LIVE * a
-            nc.sync.dma_start(planes[a][:].bitcast(I32)[0 : P - down, :], got_s[:].bitcast(I32)[down:P, :])
         load_scales(wa_s, wa_scales, range(QUADS))
-        states = [load_state(r) for r in range(2)]
+        states = [load_state(0)]
+        nc.sync.dma_start(moved_s[:].bitcast(I32)[0 : P - APART, :], got_s[:].bitcast(I32)[APART:P, :])
+        states.append(load_state(1))
         load_scales(wc_s, wc_scales, range(QUADS))
         nc.sync.dma_start(wa_w[:].bitcast(I32), wa_words.rearrange("a p n b -> p a (n b)").bitcast(I32))
         nc.sync.dma_start(wc_w[:].bitcast(I32), wc_words.rearrange("a p m -> p a m").bitcast(I32))
@@ -160,7 +158,7 @@ def tile_list_rgg_ownL_kernel(
 
         def nodes(side, a, e):
             codes = parted[side][:, a, 2 * P * e : 2 * P * (e + 1)].bitcast(FP4X4)
-            plane = planes[a][:, side * J + P * e : side * J + P * (e + 1)]
+            plane = (got_s, moved_s)[a][:, side * J + P * e : side * J + P * (e + 1)]
             return codes, plane
 
         wb_q = [quantise(weave(raw_b[a], "woven_b%d" % a), "wb%d" % a) for a in range(PASSES)]

@@ -34,9 +34,14 @@ TILES_A_HALF = HALF // P
 TGT, SRC = 0, 1
 
 BANKS = 8
-PAIR = 2
-GATED_TAGS = ("raw_b0", "raw_b1", "raw_o0", "raw_o1")
 APART = 16
+KB = 1024
+RAW_B_AT = (0, 8 * KB)
+PARTED_AT = (8 * KB, 0)
+GOT_TGT_AT = 4 * KB
+PAGE_AT = (16 * KB, 24 * KB, 32 * KB, 40 * KB)
+WOVEN_O_AT = (22 * KB, 38 * KB)
+HELD_ETA, HELD_ETA_AT = 2, 38 * KB
 
 
 def tile_list_rgg_ownL_kernel(
@@ -45,16 +50,20 @@ def tile_list_rgg_ownL_kernel(
     nc = tc.nc
     with ExitStack() as ctx:
         keep = ctx.enter_context(tc.tile_pool(name="keep", bufs=1))
+        shared = ctx.enter_context(tc.tile_pool(name="shared", bufs=1))
         psum = ctx.enter_context(tc.psum_pool(name="psum", bufs=1))
 
         def bank(b):
             return psum.tile([P, HALF], F32, name="bank", tag="bank%d" % b)
 
+        def place_at(shape, dtype, name, offset):
+            return shared.tile(shape, dtype, name=name, offset=offset, align_bytes=64)
+
         tgt_list = keep.tile([P, J // GROUP], U16, name="tgt_list")
         src_list = keep.tile([P, J // GROUP], U16, name="src_list")
         lists = (tgt_list, src_list)
-        tab_s = keep.tile([P, T], U8, name="tab_s", tag="got_w%d" % SRC, align_bytes=64)
-        tab_w = keep.tile([P, T], U32, name="tab_w", tag="tab_w", align_bytes=64)
+        tab_s = keep.tile([P, T], U8, name="tab_s", align_bytes=64)
+        tab_w = keep.tile([P, T], U32, name="tab_w", align_bytes=64)
         got_s = keep.tile([P, 2 * J], U8, name="got_s", align_bytes=64)
         moved_s = keep.tile([P, 2 * J], U8, name="moved_s", align_bytes=64)
         wa_w = keep.tile([P, PASSES, N], U32, name="wa_w", align_bytes=64)
@@ -67,22 +76,20 @@ def tile_list_rgg_ownL_kernel(
         wgo_cut = keep.tile([P, P], F32, name="wgo_cut")
 
         nc.gpsimd.memset(tab_s[:].bitcast(I32), 0)
+        nc.sync.dma_start(src_list[:], offs)
+        for r in range(LIVE):
+            (nc.sync, nc.scalar)[r % 2].dma_start(
+                tab_s[:].bitcast(I32)[r:P:APART, :],
+                tab_scales.bitcast(I32).rearrange("a (q r) w -> r q a w", r=LIVE)[r],
+            )
+        nc.sync.dma_start(tgt_list[:], offs2)
         warm = keep.tile([P, 16], F32, name="warm")
         nc.gpsimd.memset(warm[:, 0:8], 0.0)
         nc.scalar.activation(warm[:, 8:9], warm[:, 0:1], SIGMOID)
 
-        nc.gpsimd.memset(wgo_cut[:], 0.0)
         make_identity(nc, ident[:])
         for cleared in [wa_s, wc_s, moved_s]:
             nc.vector.memset(cleared[:].bitcast(I32), 0)
-
-        nc.sync.dma_start(tgt_list[:], offs2)
-        nc.sync.dma_start(src_list[:], offs)
-        for r in range(LIVE):
-            nc.sync.dma_start(
-                tab_s[:].bitcast(I32)[r:P:APART, :],
-                tab_scales.bitcast(I32).rearrange("a (q r) w -> r q a w", r=LIVE)[r],
-            )
 
         def load_scales(plane, rows, quads):
             for q in quads:
@@ -91,13 +98,11 @@ def tile_list_rgg_ownL_kernel(
                     rows.bitcast(I32)[:, LIVE * q : LIVE * (q + 1), :].rearrange("a r w -> r a w"),
                 )
 
-        def load_raw(w, a, name):
-            raw = keep.tile([P, PACK, N], F32, name="raw", tag="%s%d" % (name, a), align_bytes=64)
+        def load_raw(raw, w, a):
             nc.sync.dma_start(raw[:], w[K_PASS * a : K_PASS * (a + 1), :].rearrange("(p i) n -> p i n", i=PACK))
             return raw
 
-        def weave(raw, tag):
-            woven = keep.tile([P, N, PACK], BF16, name="woven", tag=tag, align_bytes=64)
+        def weave(woven, raw):
             nc.scalar.copy(
                 woven[:].rearrange("p (c u) i -> p c i u", u=4),
                 raw[:].rearrange("p i (c u) -> p c i u", u=4),
@@ -113,58 +118,52 @@ def tile_list_rgg_ownL_kernel(
             return codes[:].bitcast(FP8X4), plane[:]
 
         def load_state(r):
-            state = keep.tile([P, T], F32, name="state", tag="state%d" % r, align_bytes=64)
+            state = keep.tile([P, T], F32, name="state%d" % r, align_bytes=64)
             nc.sync.dma_start(state[:], rT[P * r : P * (r + 1), :])
             return state
 
-        def gather_state(state, tag):
-            own = keep.tile([P, J], F32, name="own", tag=tag, align_bytes=64)
-            nc.vector.tensor_tensor(own[:], state[:].indirect(tgt_list[:]), wgo_rows[:], MULT)
+        def gather_state(r):
+            own = keep.tile([P, J], F32, name="own%d" % r, align_bytes=64)
+            nc.vector.tensor_tensor(own[:], states[r][:].indirect(tgt_list[:]), wgo_rows[:], MULT)
             return own
 
-        def gather_scales(side):
-            nc.vector.tensor_copy(got_s[:, side * J : (side + 1) * J], tab_s[:].indirect(lists[side][:]))
-
-        def gather_words(side):
-            got_w = keep.tile([P, J], U32, name="got_w", tag="got_w%d" % side, align_bytes=64)
+        def gather_words(got_w, side):
             nc.vector.tensor_copy(got_w[:], tab_w[:].indirect(lists[side][:]))
             return got_w
 
         def part(got_w, side):
-            halves = keep.tile([P, PASSES, 2 * J], U8, name="parted%d" % side, align_bytes=64)
+            halves = place_at([P, PASSES, 2 * J], U8, "parted%d" % side, PARTED_AT[side])
             nc.vector.tensor_copy(
                 halves[:].bitcast(U16), got_w[:].bitcast(U16).rearrange("p (j a) -> p a j", a=PASSES)
             )
             return halves
 
+        def clear_page(r):
+            page = place_at([P, T], F32, "page%d" % r, PAGE_AT[r])
+            nc.gpsimd.memset(page[:].bitcast(I32), 0)
+            return page
+
         nc.sync.dma_start(tab_w[:].bitcast(I32), tab_words[0].rearrange("p t b -> p (t b)").bitcast(I32))
-        nc.sync.dma_start(wgo_cut[0:EDGE_TILES, :], wgo[0].rearrange("(e p) -> e p", p=P))
-        got = [gather_words(TGT)]
-        gather_scales(TGT)
-        gather_scales(SRC)
-        got.append(gather_words(SRC))
-        parted = [part(got[side], side) for side in (TGT, SRC)]
+        nc.sync.dma_start(wgo_cut[:], wgo[0 : P // EDGE_TILES, :].rearrange("r (e p) -> (r e) p", p=P))
+        for side in (SRC, TGT):
+            nc.vector.tensor_copy(got_s[:, side * J : (side + 1) * J], tab_s[:].indirect(lists[side][:]))
+        got_src = gather_words(keep.tile([P, J], U32, name="got_src", align_bytes=64), SRC)
 
-        raw_b = [load_raw(wb, a, "raw_b") for a in range(PASSES)]
-        raw_o = [load_raw(wo, a, "raw_o") for a in range(PASSES)]
-        load_scales(wa_s, wa_scales, range(QUADS))
-        states = [load_state(0)]
-        nc.sync.dma_start(moved_s[:].bitcast(I32)[0 : P - APART, :], got_s[:].bitcast(I32)[APART:P, :])
-        states.append(load_state(1))
-        load_scales(wc_s, wc_scales, range(QUADS))
-        nc.sync.dma_start(wa_w[:].bitcast(I32), wa_words.rearrange("a p n b -> p a (n b)").bitcast(I32))
+        raw_b = [place_at([P, PACK, N], F32, "raw_b%d" % a, RAW_B_AT[a]) for a in range(PASSES)]
+        raw_o = [keep.tile([P, PACK, N], F32, name="raw_o%d" % a, align_bytes=64) for a in range(PASSES)]
+        load_raw(raw_b[0], wb, 0)
+        load_scales(wc_s, wc_scales, (0, 1))
+        load_raw(raw_b[1], wb, 1)
+        load_scales(wc_s, wc_scales, (2, 3))
+        load_raw(raw_o[0], wo, 0)
         nc.sync.dma_start(wc_w[:].bitcast(I32), wc_words.rearrange("a p m -> p a m").bitcast(I32))
-        states = states + [load_state(r) for r in range(2, ROW_TILES)]
-
-        def nodes(side, a, e):
-            codes = parted[side][:, a, 2 * P * e : 2 * P * (e + 1)].bitcast(FP4X4)
-            plane = (got_s, moved_s)[a][:, side * J + P * e : side * J + P * (e + 1)]
-            return codes, plane
-
-        wb_q = [quantise(weave(raw_b[a], "woven_b%d" % a), "wb%d" % a) for a in range(PASSES)]
-        wo_q = [quantise(weave(raw_o[a], "woven_o%d" % a), "wo%d" % a) for a in range(PASSES)]
-        wa_q = [(wa_w[:, a, :].bitcast(FP8X4), wa_s[:, a, :]) for a in range(PASSES)]
-        wc_q = [(wc_w[:, a, :].bitcast(FP4X4), wc_s[:, a, :]) for a in range(PASSES)]
+        load_scales(wa_s, wa_scales, (0, 1))
+        nc.sync.dma_start(wa_w[:].bitcast(I32), wa_words.rearrange("a p n b -> p a (n b)").bitcast(I32))
+        load_scales(wa_s, wa_scales, (2, 3))
+        nc.sync.dma_start(moved_s[:].bitcast(I32)[0 : P - APART, :], got_s[:].bitcast(I32)[APART:P, :])
+        states = [load_state(0)]
+        load_raw(raw_o[1], wo, 1)
+        states = states + [load_state(r) for r in range(1, ROW_TILES)]
 
         turned = bank(BANKS - 1)
         nc.tensor.transpose(turned[:, 0:P], wgo_cut[:], ident[:])
@@ -176,39 +175,53 @@ def tile_list_rgg_ownL_kernel(
                 nc.tensor.transpose(spread[:, P * c : P * (c + 1)], wgo_cols[:, e : e + 1].to_broadcast([P, P]), ident[:])
             nc.scalar.copy(wgo_rows[:, HALF * h : HALF * (h + 1)], spread[:])
 
-        def passes(sums, side, w, e, steps, start, stop):
-            for a in steps:
-                codes, plane = nodes(side, a, e)
-                nc.tensor.matmul_mx(
-                    out=sums[:], lhsT=codes, lhsT_scale=plane, rhs=w[a][0], rhs_scale=w[a][1],
-                    start=start and a == 0, stop=stop and a == PASSES - 1,
-                )
+        woven_b = [
+            weave(keep.tile([P, N, PACK], BF16, name="woven_b%d" % a, align_bytes=64), raw_b[a]) for a in range(PASSES)
+        ]
+        woven_o = [weave(place_at([P, N, PACK], BF16, "woven_o0", WOVEN_O_AT[0]), raw_o[0])]
+        parted = {}
+        wb_q = [quantise(woven_b[0], "wb0")]
+        parted[SRC] = part(got_src, SRC)
+        got_tgt = gather_words(place_at([P, J], U32, "got_tgt", GOT_TGT_AT), TGT)
+        wb_q.append(quantise(woven_b[1], "wb1"))
+        parted[TGT] = part(got_tgt, TGT)
+        wo_q = [quantise(woven_o[0], "wo0")]
+        pages = [clear_page(0), clear_page(1)]
+        wa_q = [(wa_w[:, a, :].bitcast(FP8X4), wa_s[:, a, :]) for a in range(PASSES)]
+        wc_q = [(wc_w[:, a, :].bitcast(FP4X4), wc_s[:, a, :]) for a in range(PASSES)]
 
-        def weighted(target, side, w, e, b):
+        def one_pass(sums, side, w, e, a, start, stop):
+            codes = parted[side][:, a, 2 * P * e : 2 * P * (e + 1)].bitcast(FP4X4)
+            plane = (got_s, moved_s)[a][:, side * J + P * e : side * J + P * (e + 1)]
+            nc.tensor.matmul_mx(
+                out=sums[:], lhsT=codes, lhsT_scale=plane, rhs=w[a][0], rhs_scale=w[a][1], start=start, stop=stop
+            )
+
+        def product(side, w, e, b):
             sums = bank(b)
-            passes(sums, side, w, e, range(PASSES), True, True)
-            nc.scalar.activation(target, sums[:], COPY, scale=wgo_cols[:, e : e + 1])
+            for a in range(PASSES):
+                one_pass(sums, side, w, e, a, a == 0, a == PASSES - 1)
+            return sums
 
-        def open_gate(e):
-            za = bank(e % TILES_A_HALF)
-            passes(za, SRC, wb_q, e, range(PASSES), True, False)
+        def open_gate(e, b):
+            za = bank(b)
+            one_pass(za, SRC, wb_q, e, 0, True, False)
             return za
 
-        def messages(pair, za, banks):
-            eta = keep.tile([P, PAIR, N], F32, name="eta", tag="eta%d" % pair, align_bytes=64)
-            sent = keep.tile([P, PAIR, N], F32, name="sent%d" % pair)
-            for c in range(PAIR):
-                passes(za[c], TGT, wa_q, PAIR * pair + c, range(PASSES), False, True)
-                nc.scalar.activation(eta[:, c, :], za[c][:], SIGMOID)
-            for c in range(PAIR):
-                weighted(sent[:, c, :], SRC, wc_q, PAIR * pair + c, banks[c])
-            gated = keep.tile([P, PAIR, N], F32, name="gated", tag=GATED_TAGS[pair], align_bytes=64)
-            nc.vector.tensor_tensor(gated[:], sent[:], eta[:], MULT)
-            return [gated[:, c, :] for c in range(PAIR)]
+        def close_gate(za, e, eta):
+            one_pass(za, SRC, wb_q, e, 1, False, False)
+            one_pass(za, TGT, wa_q, e, 0, False, False)
+            one_pass(za, TGT, wa_q, e, 1, False, True)
+            nc.scalar.activation(eta, za[:], SIGMOID)
 
-        def projection(e):
-            kept = keep.tile([P, N], F32, name="kept%d" % e)
-            weighted(kept[:], TGT, wo_q, e, TILES_A_HALF + e % TILES_A_HALF)
+        def let_through(ms, eta, e):
+            gated = keep.tile([P, N], F32, name="gated%d" % e, align_bytes=64)
+            nc.vector.scalar_tensor_tensor(gated[:], ms[:], wgo_cols[:, e : e + 1], eta, MULT, MULT)
+            return gated[:]
+
+        def projection(e, b):
+            kept = keep.tile([P, N], F32, name="kept%d" % e, align_bytes=64)
+            nc.scalar.activation(kept[:], product(TGT, wo_q, e, b)[:], COPY, scale=wgo_cols[:, e : e + 1])
             return kept[:]
 
         def turn(target, h, r, b):
@@ -222,10 +235,13 @@ def tile_list_rgg_ownL_kernel(
                     )
             nc.scalar.copy(target, sums[:])
 
-        def place(r, halves, banks):
-            update = keep.tile([P, HALF * len(halves)], F32, name="update%d_%d" % (r, halves[0]))
+        def turned_update(r, halves, banks):
+            update = keep.tile([P, HALF * len(halves)], F32, name="update%d_%d" % (r, halves[0]), align_bytes=64)
             for i, h in enumerate(halves):
                 turn(update[:, HALF * i : HALF * (i + 1)], h, r, banks[i])
+            return update
+
+        def scatter(r, halves, update):
             lo, hi = HALF * halves[0], HALF * (halves[-1] + 1)
             nc.vector.tensor_tensor(
                 pages[r][:].indirect(tgt_list[:, lo // GROUP : hi // GROUP]), update[:], owns[r][:, lo:hi], ADD
@@ -234,29 +250,40 @@ def tile_list_rgg_ownL_kernel(
         def store(r):
             nc.sync.dma_start(out[P * r : P * (r + 1), :], pages[r][:])
 
-        owns, pages = [], []
-
-        def take_state(tag):
-            r = len(owns)
-            owns.append(gather_state(states[r], tag))
-            page = keep.tile([P, T], F32, name="page", tag="state%d" % r, align_bytes=64)
-            nc.gpsimd.memset(page[:].bitcast(I32), 0)
-            pages.append(page)
-
-        za = [open_gate(e) for e in range(4)]
-        kept = [projection(e) for e in range(4)]
-        take_state("woven_o1")
-        take_state("own1")
-        take_state("own2")
-        gated = messages(0, za[0:2], (4, 5)) + messages(1, za[2:4], (6, 7))
-        take_state("eta1")
-        place(0, [0], [4])
-        place(1, [0], [5])
-        gated = gated + messages(2, [open_gate(4), open_gate(5)], (0, 1))
-        place(2, [0], [1])
-        gated = gated + messages(3, [open_gate(6), open_gate(7)], (2, 3))
-        place(3, [0], [3])
-        kept = kept + [projection(e) for e in range(4, 8)]
-        for r in range(ROW_TILES):
-            place(r, [1], [r])
-            store(r)
+        owns = [gather_state(0)]
+        za = [open_gate(e, e) for e in range(4)]
+        ms = [product(SRC, wc_q, e, 4 + e) for e in range(4)]
+        eta = [
+            place_at([P, N], F32, "eta%d" % e, HELD_ETA_AT) if e == HELD_ETA else keep.tile([P, N], F32, name="eta%d" % e)
+            for e in range(4)
+        ]
+        for e in range(4):
+            close_gate(za[e], e, eta[e][:])
+        gated = [let_through(ms[e], eta[e][:], e) for e in range(4)]
+        owns.append(gather_state(1))
+        woven_o.append(weave(place_at([P, N, PACK], BF16, "woven_o1", WOVEN_O_AT[1]), raw_o[1]))
+        wo_q.append(quantise(woven_o[1], "wo1"))
+        pages = pages + [clear_page(2), clear_page(3)]
+        eta_late = keep.tile([P, TILES_A_HALF, N], F32, name="eta_late", align_bytes=64)
+        sent = keep.tile([P, TILES_A_HALF, N], F32, name="sent", align_bytes=64)
+        for c in range(4):
+            close_gate(open_gate(4 + c, c), 4 + c, eta_late[:, c, :])
+        for c in range(4):
+            nc.scalar.activation(sent[:, c, :], product(SRC, wc_q, 4 + c, 4 + c)[:], COPY, scale=wgo_cols[:, 4 + c : 5 + c])
+        owns.append(gather_state(2))
+        late = keep.tile([P, TILES_A_HALF, N], F32, name="late", align_bytes=64)
+        nc.vector.tensor_tensor(late[:], sent[:], eta_late[:], MULT)
+        gated = gated + [late[:, c, :] for c in range(4)]
+        owns.append(gather_state(3))
+        kept = [projection(e, e) for e in range(4)]
+        first = turned_update(0, [0], [4])
+        kept = kept + [projection(e, b) for e, b in zip(range(4, 8), (5, 6, 7, 0))]
+        scatter(0, [0], first)
+        scatter(1, [0, 1], turned_update(1, [0, 1], [1, 2]))
+        store(1)
+        scatter(2, [0, 1], turned_update(2, [0, 1], [3, 4]))
+        store(2)
+        scatter(0, [1], turned_update(0, [1], [5]))
+        store(0)
+        scatter(3, [0, 1], turned_update(3, [0, 1], [6, 7]))
+        store(3)

@@ -37,11 +37,11 @@ BANKS = 8
 APART = 16
 KB = 1024
 RAW_B_AT = (0, 8 * KB)
-PARTED_AT = (8 * KB, 0)
-GOT_TGT_AT = 4 * KB
-PAGE_AT = (16 * KB, 24 * KB, 32 * KB, 40 * KB)
-WOVEN_O_AT = (22 * KB, 38 * KB)
-HELD_ETA, HELD_ETA_AT = 2, 38 * KB
+GOT_TGT_AT = 0
+PARTED_TGT_AT = 8 * KB
+PAGE_AT = (16 * KB, 24 * KB)
+WOVEN_O1_AT = 22 * KB
+RAW_O0_AT = 32 * KB
 
 
 def tile_list_rgg_ownL_kernel(
@@ -118,7 +118,7 @@ def tile_list_rgg_ownL_kernel(
             return codes[:].bitcast(FP8X4), plane[:]
 
         def load_state(r):
-            state = keep.tile([P, T], F32, name="state%d" % r, align_bytes=64)
+            state = keep.tile([P, T], F32, name="state", tag="state%d" % r, align_bytes=64)
             nc.sync.dma_start(state[:], rT[P * r : P * (r + 1), :])
             return state
 
@@ -131,15 +131,17 @@ def tile_list_rgg_ownL_kernel(
             nc.vector.tensor_copy(got_w[:], tab_w[:].indirect(lists[side][:]))
             return got_w
 
-        def part(got_w, side):
-            halves = place_at([P, PASSES, 2 * J], U8, "parted%d" % side, PARTED_AT[side])
+        def part(halves, got_w):
             nc.vector.tensor_copy(
                 halves[:].bitcast(U16), got_w[:].bitcast(U16).rearrange("p (j a) -> p a j", a=PASSES)
             )
             return halves
 
         def clear_page(r):
-            page = place_at([P, T], F32, "page%d" % r, PAGE_AT[r])
+            if r < 2:
+                page = place_at([P, T], F32, "page%d" % r, PAGE_AT[r])
+            else:
+                page = keep.tile([P, T], F32, name="page", tag=("state3", "update0_0")[r - 2], align_bytes=64)
             nc.gpsimd.memset(page[:].bitcast(I32), 0)
             return page
 
@@ -150,20 +152,24 @@ def tile_list_rgg_ownL_kernel(
         got_src = gather_words(keep.tile([P, J], U32, name="got_src", align_bytes=64), SRC)
 
         raw_b = [place_at([P, PACK, N], F32, "raw_b%d" % a, RAW_B_AT[a]) for a in range(PASSES)]
-        raw_o = [keep.tile([P, PACK, N], F32, name="raw_o%d" % a, align_bytes=64) for a in range(PASSES)]
+        raw_o = [
+            place_at([P, PACK, N], F32, "raw_o0", RAW_O0_AT),
+            keep.tile([P, PACK, N], F32, name="raw_o1", align_bytes=64),
+        ]
         load_raw(raw_b[0], wb, 0)
         load_scales(wc_s, wc_scales, (0, 1))
-        load_raw(raw_b[1], wb, 1)
-        load_scales(wc_s, wc_scales, (2, 3))
-        load_raw(raw_o[0], wo, 0)
         nc.sync.dma_start(wc_w[:].bitcast(I32), wc_words.rearrange("a p m -> p a m").bitcast(I32))
+        load_scales(wc_s, wc_scales, (2, 3))
+        load_raw(raw_b[1], wb, 1)
+        nc.sync.dma_start(moved_s[:].bitcast(I32)[0 : P - APART, :], got_s[:].bitcast(I32)[APART:P, :])
+        states = [load_state(0)]
         load_scales(wa_s, wa_scales, (0, 1))
         nc.sync.dma_start(wa_w[:].bitcast(I32), wa_words.rearrange("a p n b -> p a (n b)").bitcast(I32))
         load_scales(wa_s, wa_scales, (2, 3))
-        nc.sync.dma_start(moved_s[:].bitcast(I32)[0 : P - APART, :], got_s[:].bitcast(I32)[APART:P, :])
-        states = [load_state(0)]
+        states.append(load_state(1))
+        load_raw(raw_o[0], wo, 0)
         load_raw(raw_o[1], wo, 1)
-        states = states + [load_state(r) for r in range(1, ROW_TILES)]
+        states = states + [load_state(r) for r in range(2, ROW_TILES)]
 
         turned = bank(BANKS - 1)
         nc.tensor.transpose(turned[:, 0:P], wgo_cut[:], ident[:])
@@ -178,15 +184,12 @@ def tile_list_rgg_ownL_kernel(
         woven_b = [
             weave(keep.tile([P, N, PACK], BF16, name="woven_b%d" % a, align_bytes=64), raw_b[a]) for a in range(PASSES)
         ]
-        woven_o = [weave(place_at([P, N, PACK], BF16, "woven_o0", WOVEN_O_AT[0]), raw_o[0])]
         parted = {}
         wb_q = [quantise(woven_b[0], "wb0")]
-        parted[SRC] = part(got_src, SRC)
+        parted[SRC] = part(keep.tile([P, PASSES, 2 * J], U8, name="parted_src", align_bytes=64), got_src)
         got_tgt = gather_words(place_at([P, J], U32, "got_tgt", GOT_TGT_AT), TGT)
         wb_q.append(quantise(woven_b[1], "wb1"))
-        parted[TGT] = part(got_tgt, TGT)
-        wo_q = [quantise(woven_o[0], "wo0")]
-        pages = [clear_page(0), clear_page(1)]
+        parted[TGT] = part(place_at([P, PASSES, 2 * J], U8, "parted_tgt", PARTED_TGT_AT), got_tgt)
         wa_q = [(wa_w[:, a, :].bitcast(FP8X4), wa_s[:, a, :]) for a in range(PASSES)]
         wc_q = [(wc_w[:, a, :].bitcast(FP4X4), wc_s[:, a, :]) for a in range(PASSES)]
 
@@ -197,10 +200,10 @@ def tile_list_rgg_ownL_kernel(
                 out=sums[:], lhsT=codes, lhsT_scale=plane, rhs=w[a][0], rhs_scale=w[a][1], start=start, stop=stop
             )
 
-        def product(side, w, e, b):
+        def product(side, w, e, b, order=(0, 1)):
             sums = bank(b)
-            for a in range(PASSES):
-                one_pass(sums, side, w, e, a, a == 0, a == PASSES - 1)
+            for a in order:
+                one_pass(sums, side, w, e, a, a == order[0], a == order[-1])
             return sums
 
         def open_gate(e, b):
@@ -236,7 +239,7 @@ def tile_list_rgg_ownL_kernel(
             nc.scalar.copy(target, sums[:])
 
         def turned_update(r, halves, banks):
-            update = keep.tile([P, HALF * len(halves)], F32, name="update%d_%d" % (r, halves[0]), align_bytes=64)
+            update = keep.tile([P, HALF * len(halves)], F32, name="update", tag="update%d_%d" % (r, halves[0]), align_bytes=64)
             for i, h in enumerate(halves):
                 turn(update[:, HALF * i : HALF * (i + 1)], h, r, banks[i])
             return update
@@ -250,40 +253,43 @@ def tile_list_rgg_ownL_kernel(
         def store(r):
             nc.sync.dma_start(out[P * r : P * (r + 1), :], pages[r][:])
 
+        def gate(za, e):
+            if e == 4:
+                eta = place_at([P, N], F32, "eta4", RAW_O0_AT)
+            else:
+                eta = keep.tile([P, N], F32, name="eta%d" % e, align_bytes=64)
+            close_gate(za, e, eta[:])
+            return eta[:]
+
+        def late_tile(e, za_bank, ms_bank):
+            eta = gate(open_gate(e, za_bank), e)
+            return let_through(product(SRC, wc_q, e, ms_bank), eta, e)
+
         owns = [gather_state(0)]
         za = [open_gate(e, e) for e in range(4)]
-        ms = [product(SRC, wc_q, e, 4 + e) for e in range(4)]
-        eta = [
-            place_at([P, N], F32, "eta%d" % e, HELD_ETA_AT) if e == HELD_ETA else keep.tile([P, N], F32, name="eta%d" % e)
-            for e in range(4)
-        ]
-        for e in range(4):
-            close_gate(za[e], e, eta[e][:])
-        gated = [let_through(ms[e], eta[e][:], e) for e in range(4)]
+        ms = [product(SRC, wc_q, e, 4 + e) for e in range(2)]
+        eta = [gate(za[e], e) for e in range(4)]
+        ms = ms + [product(SRC, wc_q, e, e - 2) for e in range(2, 4)]
+        gated = [let_through(ms[e], eta[e], e) for e in range(4)]
         owns.append(gather_state(1))
-        woven_o.append(weave(place_at([P, N, PACK], BF16, "woven_o1", WOVEN_O_AT[1]), raw_o[1]))
-        wo_q.append(quantise(woven_o[1], "wo1"))
-        pages = pages + [clear_page(2), clear_page(3)]
-        eta_late = keep.tile([P, TILES_A_HALF, N], F32, name="eta_late", align_bytes=64)
-        sent = keep.tile([P, TILES_A_HALF, N], F32, name="sent", align_bytes=64)
-        for c in range(4):
-            close_gate(open_gate(4 + c, c), 4 + c, eta_late[:, c, :])
-        for c in range(4):
-            nc.scalar.activation(sent[:, c, :], product(SRC, wc_q, 4 + c, 4 + c)[:], COPY, scale=wgo_cols[:, 4 + c : 5 + c])
+        wo_q = [quantise(weave(keep.tile([P, N, PACK], BF16, name="woven_o0", align_bytes=64), raw_o[0]), "wo0")]
+        gated = gated + [late_tile(4, 2, 4), late_tile(5, 3, 5)]
         owns.append(gather_state(2))
-        late = keep.tile([P, TILES_A_HALF, N], F32, name="late", align_bytes=64)
-        nc.vector.tensor_tensor(late[:], sent[:], eta_late[:], MULT)
-        gated = gated + [late[:, c, :] for c in range(4)]
+        wo_q.append(quantise(weave(place_at([P, N, PACK], BF16, "woven_o1", WOVEN_O1_AT), raw_o[1]), "wo1"))
+        pages = [clear_page(0), clear_page(1)]
+        gated = gated + [late_tile(6, 0, 2), late_tile(7, 1, 3)]
         owns.append(gather_state(3))
-        kept = [projection(e, e) for e in range(4)]
-        first = turned_update(0, [0], [4])
-        kept = kept + [projection(e, b) for e, b in zip(range(4, 8), (5, 6, 7, 0))]
+        pages.append(clear_page(2))
+        kept = [projection(e, b) for e, b in zip(range(4), (6, 7, 4, 5))]
+        first = turned_update(0, [0], [0])
+        kept = kept + [projection(e, b) for e, b in zip(range(4, 8), (1, 6, 7, 4))]
         scatter(0, [0], first)
-        scatter(1, [0, 1], turned_update(1, [0, 1], [1, 2]))
+        pages.append(clear_page(3))
+        scatter(1, [0, 1], turned_update(1, [0, 1], [5, 2]))
         store(1)
-        scatter(2, [0, 1], turned_update(2, [0, 1], [3, 4]))
+        scatter(2, [0, 1], turned_update(2, [0, 1], [3, 0]))
         store(2)
-        scatter(0, [1], turned_update(0, [1], [5]))
+        scatter(0, [1], turned_update(0, [1], [1]))
         store(0)
         scatter(3, [0, 1], turned_update(3, [0, 1], [6, 7]))
         store(3)

@@ -36,12 +36,11 @@ TGT, SRC = 0, 1
 BANKS = 8
 APART = 16
 KB = 1024
-RAW_B_AT = (0, 8 * KB)
-GOT_TGT_AT = 0
-PARTED_TGT_AT = 8 * KB
-PAGE_AT = (16 * KB, 24 * KB)
-WOVEN_O1_AT = 22 * KB
-RAW_O0_AT = 32 * KB
+PAGE_AT = (0, 8 * KB)
+RAW_B_AT = (4 * KB, 16 * KB)
+GOT_TGT_AT = 6 * KB
+PARTED_TGT_AT = 16 * KB
+RAW_O_AT = (24 * KB, 32 * KB)
 
 
 def tile_list_rgg_ownL_kernel(
@@ -88,7 +87,8 @@ def tile_list_rgg_ownL_kernel(
         nc.scalar.activation(warm[:, 8:9], warm[:, 0:1], SIGMOID)
 
         make_identity(nc, ident[:])
-        for cleared in [wa_s, wc_s, moved_s]:
+        first_page = keep.tile([P, T], F32, name="first_page", align_bytes=64)
+        for cleared in [wc_s, wa_s, moved_s, first_page]:
             nc.vector.memset(cleared[:].bitcast(I32), 0)
 
         def load_scales(plane, rows, quads):
@@ -123,7 +123,10 @@ def tile_list_rgg_ownL_kernel(
             return state
 
         def gather_state(r):
-            own = keep.tile([P, J], F32, name="own%d" % r, align_bytes=64)
+            if r == 2:
+                own = place_at([P, J], F32, "own%d" % r, RAW_O_AT[1] + 4 * KB)
+            else:
+                own = keep.tile([P, J], F32, name="own%d" % r, align_bytes=64)
             nc.vector.tensor_tensor(own[:], states[r][:].indirect(tgt_list[:]), wgo_rows[:], MULT)
             return own
 
@@ -137,11 +140,8 @@ def tile_list_rgg_ownL_kernel(
             )
             return halves
 
-        def clear_page(r):
-            if r < 2:
-                page = place_at([P, T], F32, "page%d" % r, PAGE_AT[r])
-            else:
-                page = keep.tile([P, T], F32, name="page", tag=("state3", "update0_0")[r - 2], align_bytes=64)
+        def clear_page(at):
+            page = place_at([P, T], F32, "page%d" % at, PAGE_AT[at])
             nc.gpsimd.memset(page[:].bitcast(I32), 0)
             return page
 
@@ -152,17 +152,14 @@ def tile_list_rgg_ownL_kernel(
         got_src = gather_words(keep.tile([P, J], U32, name="got_src", align_bytes=64), SRC)
 
         raw_b = [place_at([P, PACK, N], F32, "raw_b%d" % a, RAW_B_AT[a]) for a in range(PASSES)]
-        raw_o = [
-            place_at([P, PACK, N], F32, "raw_o0", RAW_O0_AT),
-            keep.tile([P, PACK, N], F32, name="raw_o1", align_bytes=64),
-        ]
+        raw_o = [place_at([P, PACK, N], F32, "raw_o%d" % a, RAW_O_AT[a]) for a in range(PASSES)]
         load_raw(raw_b[0], wb, 0)
         load_scales(wc_s, wc_scales, (0, 1))
         nc.sync.dma_start(wc_w[:].bitcast(I32), wc_words.rearrange("a p m -> p a m").bitcast(I32))
         load_scales(wc_s, wc_scales, (2, 3))
         load_raw(raw_b[1], wb, 1)
-        nc.sync.dma_start(moved_s[:].bitcast(I32)[0 : P - APART, :], got_s[:].bitcast(I32)[APART:P, :])
         states = [load_state(0)]
+        nc.sync.dma_start(moved_s[:].bitcast(I32)[0 : P - APART, :], got_s[:].bitcast(I32)[APART:P, :])
         load_scales(wa_s, wa_scales, (0, 1))
         nc.sync.dma_start(wa_w[:].bitcast(I32), wa_words.rearrange("a p n b -> p a (n b)").bitcast(I32))
         load_scales(wa_s, wa_scales, (2, 3))
@@ -254,8 +251,8 @@ def tile_list_rgg_ownL_kernel(
             nc.sync.dma_start(out[P * r : P * (r + 1), :], pages[r][:])
 
         def gate(za, e):
-            if e == 4:
-                eta = place_at([P, N], F32, "eta4", RAW_O0_AT)
+            if e in (4, 5):
+                eta = place_at([P, N], F32, "eta%d" % e, RAW_O_AT[1] + 2 * KB * (e - 4))
             else:
                 eta = keep.tile([P, N], F32, name="eta%d" % e, align_bytes=64)
             close_gate(za, e, eta[:])
@@ -265,6 +262,8 @@ def tile_list_rgg_ownL_kernel(
             eta = gate(open_gate(e, za_bank), e)
             return let_through(product(SRC, wc_q, e, ms_bank), eta, e)
 
+        pages = [first_page, clear_page(0), clear_page(1)]
+        pages.append(pages[2])
         owns = [gather_state(0)]
         za = [open_gate(e, e) for e in range(4)]
         ms = [product(SRC, wc_q, e, 4 + e) for e in range(2)]
@@ -273,23 +272,22 @@ def tile_list_rgg_ownL_kernel(
         gated = [let_through(ms[e], eta[e], e) for e in range(4)]
         owns.append(gather_state(1))
         wo_q = [quantise(weave(keep.tile([P, N, PACK], BF16, name="woven_o0", align_bytes=64), raw_o[0]), "wo0")]
-        gated = gated + [late_tile(4, 2, 4), late_tile(5, 3, 5)]
+        gated.append(late_tile(4, 2, 4))
+        wo_q.append(quantise(weave(keep.tile([P, N, PACK], BF16, name="woven_o1", align_bytes=64), raw_o[1]), "wo1"))
         owns.append(gather_state(2))
-        wo_q.append(quantise(weave(place_at([P, N, PACK], BF16, "woven_o1", WOVEN_O1_AT), raw_o[1]), "wo1"))
-        pages = [clear_page(0), clear_page(1)]
-        gated = gated + [late_tile(6, 0, 2), late_tile(7, 1, 3)]
+        gated = gated + [late_tile(5, 3, 5), late_tile(6, 0, 2), late_tile(7, 1, 3)]
         owns.append(gather_state(3))
-        pages.append(clear_page(2))
-        kept = [projection(e, b) for e, b in zip(range(4), (6, 7, 4, 5))]
+        kept = [projection(e, b) for e, b in zip(range(4), (6, 7, 4, 6))]
         first = turned_update(0, [0], [0])
-        kept = kept + [projection(e, b) for e, b in zip(range(4, 8), (1, 6, 7, 4))]
+        second = turned_update(1, [0], [1])
+        kept = kept + [projection(e, b) for e, b in zip(range(4, 8), (7, 4, 5, 2))]
         scatter(0, [0], first)
-        pages.append(clear_page(3))
-        scatter(1, [0, 1], turned_update(1, [0, 1], [5, 2]))
-        store(1)
-        scatter(2, [0, 1], turned_update(2, [0, 1], [3, 0]))
+        scatter(1, [0], second)
+        scatter(2, [0, 1], turned_update(2, [0, 1], [3, 6]))
         store(2)
-        scatter(0, [1], turned_update(0, [1], [1]))
+        scatter(0, [1], turned_update(0, [1], [0]))
         store(0)
-        scatter(3, [0, 1], turned_update(3, [0, 1], [6, 7]))
+        scatter(1, [1], turned_update(1, [1], [1]))
+        store(1)
+        scatter(3, [0, 1], turned_update(3, [0, 1], [7, 4]))
         store(3)

from contextlib import ExitStack

import concourse.mybir as mybir
from concourse.masks import make_identity

K, N, T, J = 1024, 512, 2048, 1024
FLOPS = 4 * 2 * K * N * J

F32 = mybir.dt.float32
BF16 = mybir.dt.bfloat16
I32 = mybir.dt.int32
U32 = mybir.dt.uint32
U16 = mybir.dt.uint16
U8 = mybir.dt.uint8
FP8X4 = mybir.dt.float8_e4m3fn_x4
FP4X4 = mybir.dt.float4_e2m1fn_x4
MULT = mybir.AluOpType.mult
ADD = mybir.AluOpType.add
COPY = mybir.ActivationFunctionType.Copy
SIGMOID = mybir.ActivationFunctionType.Sigmoid

P = 128
PACK = 4
K_PASS = P * PACK
PASSES = K // K_PASS
QUAD = 32
QUADS = P // QUAD
LIVE = 4
GROUP = 16
EDGE_TILES = J // P
ROW_TILES = N // P
HALF = 512
TILES_A_HALF = HALF // P
TGT, SRC = 0, 1

BANKS = 8
APART = 16
KB = 1024
PAGE_AT = (0, 8 * KB)
RAW_B_AT = (4 * KB, 16 * KB)
GOT_TGT_AT = 6 * KB
PARTED_TGT_AT = 16 * KB
RAW_O_AT = (24 * KB, 32 * KB)


def tile_list_rgg_ownL_kernel(
    tc, tab_words, tab_scales, wa_words, wa_scales, wb, wc_words, wc_scales, wo, rT, wgo, offs, offs2, out
):
    nc = tc.nc
    with ExitStack() as ctx:
        keep = ctx.enter_context(tc.tile_pool(name="keep", bufs=1))
        shared = ctx.enter_context(tc.tile_pool(name="shared", bufs=1))
        psum = ctx.enter_context(tc.psum_pool(name="psum", bufs=1))

        def bank(b):
            return psum.tile([P, HALF], F32, name="bank", tag="bank%d" % b)

        def place_at(shape, dtype, name, offset):
            return shared.tile(shape, dtype, name=name, offset=offset, align_bytes=64)

        tgt_list = keep.tile([P, J // GROUP], U16, name="tgt_list")
        src_list = keep.tile([P, J // GROUP], U16, name="src_list")
        lists = (tgt_list, src_list)
        tab_s = keep.tile([P, T], U8, name="tab_s", align_bytes=64)
        tab_w = keep.tile([P, T], U32, name="tab_w", align_bytes=64)
        got_s = keep.tile([P, 2 * J], U8, name="got_s", align_bytes=64)
        moved_s = keep.tile([P, 2 * J], U8, name="moved_s", align_bytes=64)
        wa_w = keep.tile([P, PASSES, N], U32, name="wa_w", align_bytes=64)
        wc_w = keep.tile([P, PASSES, 2 * N], U8, name="wc_w", align_bytes=64)
        wa_s = keep.tile([P, PASSES, N], U8, name="wa_s", align_bytes=64)
        wc_s = keep.tile([P, PASSES, N], U8, name="wc_s", align_bytes=64)
        wgo_rows = keep.tile([P, J], F32, name="wgo_rows")
        wgo_cols = keep.tile([P, EDGE_TILES], F32, name="wgo_cols")
        ident = keep.tile([P, P], F32, name="ident")
        wgo_cut = keep.tile([P, P], F32, name="wgo_cut")

        nc.gpsimd.memset(tab_s[:].bitcast(I32), 0)
        nc.sync.dma_start(src_list[:], offs)
        for r in range(LIVE):
            (nc.sync, nc.scalar)[r % 2].dma_start(
                tab_s[:].bitcast(I32)[r:P:APART, :],
                tab_scales.bitcast(I32).rearrange("a (q r) w -> r q a w", r=LIVE)[r],
            )
        nc.sync.dma_start(tgt_list[:], offs2)
        warm = keep.tile([P, 16], F32, name="warm")
        nc.gpsimd.memset(warm[:, 0:8], 0.0)
        nc.scalar.activation(warm[:, 8:9], warm[:, 0:1], SIGMOID)

        make_identity(nc, ident[:])
        first_page = keep.tile([P, T], F32, name="first_page", align_bytes=64)
        for cleared in [wc_s, wa_s, moved_s, first_page]:
            nc.vector.memset(cleared[:].bitcast(I32), 0)

        def load_scales(plane, rows, quads):
            for q in quads:
                nc.sync.dma_start(
                    plane[:].bitcast(I32)[QUAD * q : QUAD * q + LIVE, :, :],
                    rows.bitcast(I32)[:, LIVE * q : LIVE * (q + 1), :].rearrange("a r w -> r a w"),
                )

        def load_raw(raw, w, a):
            nc.sync.dma_start(raw[:], w[K_PASS * a : K_PASS * (a + 1), :].rearrange("(p i) n -> p i n", i=PACK))
            return raw

        def weave(woven, raw):
            nc.scalar.copy(
                woven[:].rearrange("p (c u) i -> p c i u", u=4),
                raw[:].rearrange("p i (c u) -> p c i u", u=4),
            )
            return woven

        def quantise(woven, name):
            codes = keep.tile([P, N], U32, name=name + "_w", align_bytes=64)
            plane = keep.tile([P, N], U8, name=name + "_s", align_bytes=64)
            nc.vector.quantize_mx(
                out=codes[:].bitcast(FP8X4), scales=plane[:], in_=woven[:].rearrange("p n i -> p (n i)")
            )
            return codes[:].bitcast(FP8X4), plane[:]

        def load_state(r):
            state = keep.tile([P, T], F32, name="state", tag="state%d" % r, align_bytes=64)
            nc.sync.dma_start(state[:], rT[P * r : P * (r + 1), :])
            return state

        def gather_state(r):
            if r == 2:
                own = place_at([P, J], F32, "own%d" % r, RAW_O_AT[1] + 4 * KB)
            else:
                own = keep.tile([P, J], F32, name="own%d" % r, align_bytes=64)
            nc.vector.tensor_tensor(own[:], states[r][:].indirect(tgt_list[:]), wgo_rows[:], MULT)
            return own

        def gather_words(got_w, side):
            nc.vector.tensor_copy(got_w[:], tab_w[:].indirect(lists[side][:]))
            return got_w

        def part(halves, got_w):
            nc.vector.tensor_copy(
                halves[:].bitcast(U16), got_w[:].bitcast(U16).rearrange("p (j a) -> p a j", a=PASSES)
            )
            return halves

        def clear_page(at):
            page = place_at([P, T], F32, "page%d" % at, PAGE_AT[at])
            nc.gpsimd.memset(page[:].bitcast(I32), 0)
            return page

        nc.sync.dma_start(tab_w[:].bitcast(I32), tab_words[0].rearrange("p t b -> p (t b)").bitcast(I32))
        nc.sync.dma_start(wgo_cut[:], wgo[0 : P // EDGE_TILES, :].rearrange("r (e p) -> (r e) p", p=P))
        for side in (SRC, TGT):
            nc.vector.tensor_copy(got_s[:, side * J : (side + 1) * J], tab_s[:].indirect(lists[side][:]))
        got_src = gather_words(keep.tile([P, J], U32, name="got_src", align_bytes=64), SRC)

        raw_b = [place_at([P, PACK, N], F32, "raw_b%d" % a, RAW_B_AT[a]) for a in range(PASSES)]
        raw_o = [place_at([P, PACK, N], F32, "raw_o%d" % a, RAW_O_AT[a]) for a in range(PASSES)]
        load_raw(raw_b[0], wb, 0)
        load_scales(wc_s, wc_scales, (0, 1))
        nc.sync.dma_start(wc_w[:].bitcast(I32), wc_words.rearrange("a p m -> p a m").bitcast(I32))
        load_scales(wc_s, wc_scales, (2, 3))
        load_raw(raw_b[1], wb, 1)
        states = [load_state(0)]
        nc.sync.dma_start(moved_s[:].bitcast(I32)[0 : P - APART, :], got_s[:].bitcast(I32)[APART:P, :])
        load_scales(wa_s, wa_scales, (0, 1))
        nc.sync.dma_start(wa_w[:].bitcast(I32), wa_words.rearrange("a p n b -> p a (n b)").bitcast(I32))
        load_scales(wa_s, wa_scales, (2, 3))
        states.append(load_state(1))
        load_raw(raw_o[0], wo, 0)
        load_raw(raw_o[1], wo, 1)
        states = states + [load_state(r) for r in range(2, ROW_TILES)]

        turned = bank(BANKS - 1)
        nc.tensor.transpose(turned[:, 0:P], wgo_cut[:], ident[:])
        nc.scalar.copy(wgo_cols[:], turned[:, 0:EDGE_TILES])
        for h in range(J // HALF):
            spread = bank(BANKS - 2 - h)
            for c in range(TILES_A_HALF):
                e = TILES_A_HALF * h + c
                nc.tensor.transpose(spread[:, P * c : P * (c + 1)], wgo_cols[:, e : e + 1].to_broadcast([P, P]), ident[:])
            nc.scalar.copy(wgo_rows[:, HALF * h : HALF * (h + 1)], spread[:])

        woven_b = [
            weave(keep.tile([P, N, PACK], BF16, name="woven_b%d" % a, align_bytes=64), raw_b[a]) for a in range(PASSES)
        ]
        parted = {}
        wb_q = [quantise(woven_b[0], "wb0")]
        parted[SRC] = part(keep.tile([P, PASSES, 2 * J], U8, name="parted_src", align_bytes=64), got_src)
        got_tgt = gather_words(place_at([P, J], U32, "got_tgt", GOT_TGT_AT), TGT)
        wb_q.append(quantise(woven_b[1], "wb1"))
        parted[TGT] = part(place_at([P, PASSES, 2 * J], U8, "parted_tgt", PARTED_TGT_AT), got_tgt)
        wa_q = [(wa_w[:, a, :].bitcast(FP8X4), wa_s[:, a, :]) for a in range(PASSES)]
        wc_q = [(wc_w[:, a, :].bitcast(FP4X4), wc_s[:, a, :]) for a in range(PASSES)]

        def one_pass(sums, side, w, e, a, start, stop):
            codes = parted[side][:, a, 2 * P * e : 2 * P * (e + 1)].bitcast(FP4X4)
            plane = (got_s, moved_s)[a][:, side * J + P * e : side * J + P * (e + 1)]
            nc.tensor.matmul_mx(
                out=sums[:], lhsT=codes, lhsT_scale=plane, rhs=w[a][0], rhs_scale=w[a][1], start=start, stop=stop
            )

        def product(side, w, e, b, order=(0, 1)):
            sums = bank(b)
            for a in order:
                one_pass(sums, side, w, e, a, a == order[0], a == order[-1])
            return sums

        def open_gate(e, b):
            za = bank(b)
            one_pass(za, SRC, wb_q, e, 0, True, False)
            return za

        def close_gate(za, e, eta):
            one_pass(za, SRC, wb_q, e, 1, False, False)
            one_pass(za, TGT, wa_q, e, 0, False, False)
            one_pass(za, TGT, wa_q, e, 1, False, True)
            nc.scalar.activation(eta, za[:], SIGMOID)

        def let_through(ms, eta, e):
            gated = keep.tile([P, N], F32, name="gated%d" % e, align_bytes=64)
            nc.vector.scalar_tensor_tensor(gated[:], ms[:], wgo_cols[:, e : e + 1], eta, MULT, MULT)
            return gated[:]

        def projection(e, b):
            kept = keep.tile([P, N], F32, name="kept%d" % e, align_bytes=64)
            nc.scalar.activation(kept[:], product(TGT, wo_q, e, b)[:], COPY, scale=wgo_cols[:, e : e + 1])
            return kept[:]

        def turn(target, h, r, b):
            sums = bank(b)
            for c in range(TILES_A_HALF):
                e = TILES_A_HALF * h + c
                for s, term in enumerate((gated[e], kept[e])):
                    nc.tensor.matmul(
                        sums[:, P * c : P * (c + 1)], term[:, P * r : P * (r + 1)], ident[:],
                        start=(s == 0), stop=(s == 1), is_transpose=True,
                    )
            nc.scalar.copy(target, sums[:])

        def turned_update(r, halves, banks):
            update = keep.tile([P, HALF * len(halves)], F32, name="update", tag="update%d_%d" % (r, halves[0]), align_bytes=64)
            for i, h in enumerate(halves):
                turn(update[:, HALF * i : HALF * (i + 1)], h, r, banks[i])
            return update

        def scatter(r, halves, update):
            lo, hi = HALF * halves[0], HALF * (halves[-1] + 1)
            nc.vector.tensor_tensor(
                pages[r][:].indirect(tgt_list[:, lo // GROUP : hi // GROUP]), update[:], owns[r][:, lo:hi], ADD
            )

        def store(r):
            nc.sync.dma_start(out[P * r : P * (r + 1), :], pages[r][:])

        def gate(za, e):
            if e in (4, 5):
                eta = place_at([P, N], F32, "eta%d" % e, RAW_O_AT[1] + 2 * KB * (e - 4))
            else:
                eta = keep.tile([P, N], F32, name="eta%d" % e, align_bytes=64)
            close_gate(za, e, eta[:])
            return eta[:]

        def late_tile(e, za_bank, ms_bank):
            eta = gate(open_gate(e, za_bank), e)
            return let_through(product(SRC, wc_q, e, ms_bank), eta, e)

        pages = [first_page, clear_page(0), clear_page(1)]
        pages.append(pages[2])
        owns = [gather_state(0)]
        za = [open_gate(e, e) for e in range(4)]
        ms = [product(SRC, wc_q, e, 4 + e) for e in range(2)]
        eta = [gate(za[e], e) for e in range(4)]
        ms = ms + [product(SRC, wc_q, e, e - 2) for e in range(2, 4)]
        gated = [let_through(ms[e], eta[e], e) for e in range(4)]
        owns.append(gather_state(1))
        wo_q = [quantise(weave(keep.tile([P, N, PACK], BF16, name="woven_o0", align_bytes=64), raw_o[0]), "wo0")]
        gated.append(late_tile(4, 2, 4))
        wo_q.append(quantise(weave(keep.tile([P, N, PACK], BF16, name="woven_o1", align_bytes=64), raw_o[1]), "wo1"))
        owns.append(gather_state(2))
        gated = gated + [late_tile(5, 3, 5), late_tile(6, 0, 2), late_tile(7, 1, 3)]
        owns.append(gather_state(3))
        kept = [projection(e, b) for e, b in zip(range(4), (6, 7, 4, 6))]
        first = turned_update(0, [0], [0])
        second = turned_update(1, [0], [1])
        kept = kept + [projection(e, b) for e, b in zip(range(4, 8), (7, 4, 5, 2))]
        scatter(0, [0], first)
        scatter(1, [0], second)
        scatter(2, [0, 1], turned_update(2, [0, 1], [3, 6]))
        store(2)
        scatter(0, [1], turned_update(0, [1], [0]))
        store(0)
        scatter(1, [1], turned_update(1, [1], [1]))
        store(1)
        scatter(3, [0, 1], turned_update(3, [0, 1], [7, 4]))
        store(3)
